import numpy as np
import ml_dtypes


def mxq(x, axis, fmt="e4m3"):
    dtype, down = {"e4m3": (ml_dtypes.float8_e4m3fn, 7), "e5m2": (ml_dtypes.float8_e5m2, 14)}[fmt]
    v = np.moveaxis(np.asarray(x, np.float32).astype(ml_dtypes.bfloat16).astype(np.float64), axis, -1)
    blocks = v.reshape(v.shape[:-1] + (-1, 32))
    amax = np.abs(blocks).max(-1, keepdims=True)
    byte = np.maximum(np.where(amax > 0, np.frexp(amax)[1] - 1 + 127, 0) - down, 1)
    scale = np.exp2(byte - 127.0)
    codes = (blocks / scale).astype(np.float32).astype(dtype).astype(np.float64)
    return np.moveaxis((codes * scale).reshape(v.shape), -1, axis)


WIDE = False


def mx_kscale(k):
    if not WIDE:
        return np.ones(k)
    levels = np.array([10, -10, 5, -5, 0])
    if k % 512:
        return np.exp2(np.random.permutation(np.resize(levels, k // 32))).repeat(32)
    a = np.empty((k // 512, 16))
    for p in range(k // 512):
        a[p, :8] = np.random.permutation(np.resize(levels, 8))
        for g in range(8):
            far = levels[np.abs(levels - a[p, g]) >= 10]
            a[p, g + 8] = far[np.random.randint(len(far))]
    return np.exp2(a.ravel()).repeat(32)


def f64(x):
    return np.asarray(x).astype(np.float64)


E2M1 = np.array([0.0, 0.5, 1.0, 1.5, 2.0, 3.0, 4.0, 6.0, -0.0, -0.5, -1.0, -1.5, -2.0, -3.0, -4.0, -6.0])


def pack_weight(w, fmt):
    k, n = w.shape
    w = f64(np.asarray(w, np.float32).astype(ml_dtypes.bfloat16)).reshape(k // 32, 32, n)
    amax = np.abs(w).max(1)
    if fmt == "e4m3":
        byte = np.frexp(amax)[1] - 1 + 127 - 7
    else:
        mant, ex = np.frexp(amax / 6.0)
        byte = np.where(mant > 0.5, ex, ex - 1) + 127
    byte = np.clip(np.where(amax > 0, byte, 1), 1, 254)
    scaled = (w * np.exp2(127.0 - byte)[:, None, :]).reshape(k, n).astype(np.float32)
    by_word = np.ascontiguousarray(scaled.reshape(k // 512, 128, 4, n).transpose(0, 1, 3, 2))
    if fmt == "e4m3":
        words = by_word.astype(ml_dtypes.float8_e4m3fn).view(np.uint8)
    else:
        c = by_word.astype(ml_dtypes.float4_e2m1fn).view(np.uint8) & 0xF
        words = (c[..., 0::2] | (c[..., 1::2] << 4)).reshape(k // 512, 128, 2 * n)
    return np.ascontiguousarray(words), np.ascontiguousarray(byte.astype(np.uint8).reshape(k // 512, 16, n))


def unpack_weight(words, scales, fmt):
    g, _, n = scales.shape
    words = np.ascontiguousarray(words).reshape(g, 128, n, -1)
    if fmt == "e4m3":
        vals = words.view(ml_dtypes.float8_e4m3fn).astype(np.float64)
    else:
        nib = np.empty((g, 128, n, 4), np.uint8)
        nib[..., 0::2] = words & 0xF
        nib[..., 1::2] = words >> 4
        vals = E2M1[nib]
    vals = vals * np.repeat(np.exp2(scales.astype(np.float64) - 127.0), 8, axis=1)[..., None]
    return vals.transpose(0, 1, 3, 2).reshape(g * 512, n)


O, K, R, M, T = 1024, 2048, 512, 1024, 1024


def setup_inputs():
    n = np.random.standard_normal
    s = mx_kscale(K)[:, None]
    u = mx_kscale(R)[:, None]
    x = n((K, T)); x[:O] *= 6.0
    w = n((K, M)) / np.sqrt(K) / s; w[:O] /= 2.0
    p_w8 = pack_weight(w[:O], "e4m3")
    p_w4 = pack_weight(w[O:], "e2m1")
    p_up = pack_weight(n((R, M)) / np.sqrt(R) / u, "e2m1")
    return {
        "x": (x * s).astype(np.float32),
        "w8_words": p_w8[0],
        "w8_scales": p_w8[1],
        "w4_words": p_w4[0],
        "w4_scales": p_w4[1],
        "down": (0.3 * n((K, R)) / np.sqrt(K) / s * u.T).astype(np.float32),
        "up_words": p_up[0],
        "up_scales": p_up[1],
        "prev": (n((1024, 1024))).astype(np.float32),
    }


def reference(x, w8_words, w8_scales, w4_words, w4_scales, down, up_words, up_scales, prev):
    x_ = mxq(f64(x), 0, "e4m3")
    w8_ = unpack_weight(w8_words, w8_scales, "e4m3")
    w4_ = unpack_weight(w4_words, w4_scales, "e2m1")
    down_ = mxq(f64(down), 0, "e4m3")
    up_ = unpack_weight(up_words, up_scales, "e2m1")
    h_ = mxq(down_.T @ x_, 0, "e4m3")
    y = x_[:O].T @ w8_ + x_[O:].T @ w4_ + h_.T @ up_
    return f64(prev) + y

@@ -1,0 +1,394 @@
+from contextlib import ExitStack
+
+import concourse.mybir as mybir
+
+O, K, R, M, T = 1024, 2048, 512, 1024, 1024
+FLOPS = 2 * T * (K * R + K * M + R * M)
+BYTES = 4 * (K * T + K * R + 2 * T * M) + O * M + (K - O) * M // 2 + R * M // 2 + (K + R) * M // 32
+
+F32 = mybir.dt.float32
+BF16 = mybir.dt.bfloat16
+U32 = mybir.dt.uint32
+I32 = mybir.dt.int32
+U8 = mybir.dt.uint8
+FP8X4 = mybir.dt.float8_e4m3fn_x4
+FP4X4 = mybir.dt.float4_e2m1fn_x4
+ADD = mybir.AluOpType.add
+
+P = 128
+PACK = 4
+K_PASS = P * PACK
+N_TILE = 512
+GROUPS = K // K_PASS
+SLICES = ((0, 256), (256, 256), (512, 512))
+W_MAX = 512
+Y_BANKS = ("a0", "a1"), ("a2", "a3"), ("b0", "b1"), ("a0", "a1"), ("b0", "b1"), ("a0", "a1"), ("a2", "a3"), ("b2", "b3")
+H_BANKS = ("b0", "b1", "b2", "b3"), ("b2", "b2", "b3", "b3"), ("a2", "a3", "b2", "b3")
+
+
+def tile_mix_three_tm_res_kernel(
+    tc, x, w8_words, w8_scales, w4_words, w4_scales, down, up_words, up_scales, prev, out
+):
+    nc = tc.nc
+    with ExitStack() as ctx:
+        keep = ctx.enter_context(tc.tile_pool(name="keep", bufs=1))
+        xraw = ctx.enter_context(tc.tile_pool(name="xraw", bufs=1))
+        draw = ctx.enter_context(tc.tile_pool(name="draw", bufs=4))
+        group = ctx.enter_context(tc.tile_pool(name="group", bufs=3))
+        hsb = ctx.enter_context(tc.tile_pool(name="hsb", bufs=1))
+        psum = ctx.enter_context(tc.psum_pool(name="psum", bufs=1))
+        ctx.enter_context(tc.manual_schedule())
+
+        w8 = keep.tile([P, 2, M], U32, name="w8", align_bytes=64)
+        w4 = keep.tile([P, 2, 2 * M], U8, name="w4", align_bytes=64)
+        up = keep.tile([P, 2 * M], U8, name="up", align_bytes=64)
+        sc = keep.tile([P, 5, M], U8, name="sc", align_bytes=64)
+        xq, xs, xr = {}, {}, {}
+        dq, ds, dr = {}, {}, {}
+        for s, (t0, w) in enumerate(SLICES):
+            for g in range(GROUPS):
+                xq[s, g] = keep.tile([P, w], U32, name=f"xq{s}{g}", align_bytes=64)
+                xs[s, g] = keep.tile([P, w], U8, name=f"xs{s}{g}", align_bytes=64)
+        for g in range(GROUPS):
+            dq[g] = keep.tile([P, R], U32, name=f"dq{g}", align_bytes=64)
+            ds[g] = keep.tile([P, R], U8, name=f"ds{g}", align_bytes=64)
+        pv = [keep.tile([P, 2, M], F32, name=f"pv{b}") for b in range(4)]
+
+        def load_x(s, g):
+            t0, w = SLICES[s]
+            xr[s, g] = xraw.tile([P, PACK, w], F32, name=f"xr{s}{g}")
+            rows = x[g * K_PASS : (g + 1) * K_PASS, t0 : t0 + w]
+            nc.sync.dma_start(out=xr[s, g][:], in_=rows.rearrange("(p j) w -> p j w", j=PACK))
+
+        def load_d(g):
+            dr[g] = draw.tile([P, PACK, R], F32, name="dr")
+            rows = down[g * K_PASS : (g + 1) * K_PASS, :]
+            nc.sync.dma_start(out=dr[g][:], in_=rows.rearrange("(p j) r -> p j r", j=PACK))
+
+        def load_w8(a):
+            nc.sync.dma_start(
+                out=w8[:, a, :].bitcast(I32), in_=w8_words[a].rearrange("p n i -> p (n i)").bitcast(I32)
+            )
+
+        def load_w4():
+            nc.sync.dma_start(out=w4[:].bitcast(I32), in_=w4_words.rearrange("a p n -> p a n").bitcast(I32))
+
+        def load_up():
+            nc.sync.dma_start(out=up[:].bitcast(I32), in_=up_words[0].bitcast(I32))
+
+        def load_scales(which, r):
+            if which == 2:
+                dst = sc[r:P:32, 4, :]
+                src = up_scales[0].rearrange("(q r) n -> r q n", r=4)[r]
+            else:
+                scales = (w8_scales, w4_scales)[which]
+                dst = sc[r:P:32, 2 * which : 2 * which + 2, :]
+                src = scales.rearrange("a (q r) n -> r q a n", r=4)[r]
+            nc.sync.dma_start(out=dst.bitcast(I32), in_=src.bitcast(I32))
+
+        def load_prev(b):
+            rows = prev[b * 256 : (b + 1) * 256, :]
+            nc.sync.dma_start(out=pv[b][:], in_=rows.rearrange("(a p) n -> p a n", p=P))
+
+        def store(t):
+            nc.sync.dma_start(out=out[t * P : (t + 1) * P, :], in_=pv[t // 2][:, t % 2, :])
+
+        def store_half(t, n):
+            n_cols = slice(n * N_TILE, (n + 1) * N_TILE)
+            nc.sync.dma_start(out=out[t * P : (t + 1) * P, n_cols], in_=pv[t // 2][:, t % 2, n_cols])
+
+        xb, db = {}, {}
+
+        def new_xb(s, g):
+            xb[s, g] = group.tile([P, PACK * W_MAX], BF16, name="xb", align_bytes=64)
+
+        def four(dst, src, c0, c1):
+            o = dst[:, PACK * c0 : PACK * c1].rearrange("p (c j) -> p c j", j=PACK)
+            i = src[:, :, c0:c1].rearrange("p j c -> p c j")
+            return o, i
+
+        def cast_x(s, g, eng, c0, c1):
+            o, i = four(xb[s, g], xr[s, g], c0, c1)
+            if eng == "v":
+                nc.vector.tensor_copy(out=o, in_=i)
+            else:
+                nc.scalar.copy(out=o, in_=i)
+
+        def quant_x(s, g):
+            w = SLICES[s][1]
+            parts = ((0, 128), (128, 256)) if w == 256 else ((0, w),)
+            for c0, c1 in parts:
+                nc.vector.quantize_mx(
+                    out=xq[s, g][:, c0:c1].bitcast(FP8X4),
+                    scales=xs[s, g][:, c0:c1],
+                    in_=xb[s, g][:, PACK * c0 : PACK * c1],
+                )
+
+        def new_db(g):
+            db[g] = group.tile([P, PACK * R], BF16, name="db", align_bytes=64)
+
+        def cast_d(g, eng, m0, m1):
+            o = db[g][:].rearrange("p (t m j) -> p m t j", t=4, j=PACK)[:, m0:m1]
+            i = dr[g][:].rearrange("p j (m t) -> p m t j", t=4)[:, m0:m1]
+            if eng == "v":
+                nc.vector.tensor_copy(out=o, in_=i)
+            else:
+                nc.scalar.copy(out=o, in_=i)
+
+        def quant_d(g):
+            nc.vector.quantize_mx(out=dq[g][:].bitcast(FP8X4), scales=ds[g][:], in_=db[g][:])
+
+        hp, hf, hb, hq, hs = {}, {}, {}, {}, {}
+
+        def h_mm(s, j, g):
+            w = SLICES[s][1]
+            shared = s == 1
+            if g == 0 and not (shared and j % 2):
+                hp[s, j] = psum.tile([P, W_MAX], F32, name=H_BANKS[s][j])
+                if shared:
+                    hp[s, j + 1] = hp[s, j]
+            c0 = w * (j % 2) if shared else 0
+            cols = slice(j * P, (j + 1) * P)
+            nc.tensor.matmul_mx(
+                out=hp[s, j][:, c0 : c0 + w],
+                lhsT=dq[g][:, cols].bitcast(FP8X4),
+                lhsT_scale=ds[g][:, cols],
+                rhs=xq[s, g][:].bitcast(FP8X4),
+                rhs_scale=xs[s, g][:],
+                start=(g == 0),
+                stop=(g == GROUPS - 1),
+            )
+
+        def h_new(s):
+            w = SLICES[s][1]
+            hf[s] = hsb.tile([P, PACK, w], F32, name="hf")
+            hb[s] = hsb.tile([P, PACK * W_MAX], BF16, name="hb", align_bytes=64)
+            hq[s] = keep.tile([P, w], U32, name=f"hq{s}", align_bytes=64)
+            hs[s] = keep.tile([P, w], U8, name=f"hs{s}", align_bytes=64)
+
+        def h_evac(s, j, eng="s"):
+            w = SLICES[s][1]
+            if s == 1:
+                dst, src = hf[s][:, j : j + 2, :].rearrange("p j w -> p (j w)"), hp[s, j][:]
+            else:
+                dst, src = hf[s][:, j, :], hp[s, j][:, :w]
+            if eng == "s":
+                nc.scalar.copy(out=dst, in_=src)
+            else:
+                nc.vector.tensor_copy(out=dst, in_=src)
+
+        def h_inter(s, eng, c0, c1):
+            o, i = four(hb[s], hf[s], c0, c1)
+            if eng == "v":
+                nc.vector.tensor_copy(out=o, in_=i)
+            else:
+                nc.scalar.copy(out=o, in_=i)
+
+        def h_quant(s):
+            w = SLICES[s][1]
+            nc.vector.quantize_mx(out=hq[s][:].bitcast(FP8X4), scales=hs[s][:], in_=hb[s][:, : PACK * w])
+
+        yp = {}
+
+        def where(t):
+            for s, (t0, w) in enumerate(SLICES):
+                if t0 <= t * P < t0 + w:
+                    return s, t * P - t0
+
+        def y_w(t, n, g):
+            s, c = where(t)
+            cols = slice(c, c + P)
+            n_cols = slice(n * N_TILE, (n + 1) * N_TILE)
+            if g == 0:
+                yp[t, n] = psum.tile([P, N_TILE], F32, name=Y_BANKS[t][n])
+            if g < 2:
+                rhs = w8[:, g, n_cols].bitcast(FP8X4)
+            else:
+                rhs = w4[:, g - 2, 2 * n * N_TILE : 2 * (n + 1) * N_TILE].bitcast(FP4X4)
+            nc.tensor.matmul_mx(
+                out=yp[t, n][:],
+                lhsT=xq[s, g][:, cols].bitcast(FP8X4),
+                lhsT_scale=xs[s, g][:, cols],
+                rhs=rhs,
+                rhs_scale=sc[:, g, n_cols],
+                start=(g == 0),
+                stop=False,
+            )
+
+        def y_up(t, n):
+            s, c = where(t)
+            cols = slice(c, c + P)
+            n_cols = slice(n * N_TILE, (n + 1) * N_TILE)
+            nc.tensor.matmul_mx(
+                out=yp[t, n][:],
+                lhsT=hq[s][:, cols].bitcast(FP8X4),
+                lhsT_scale=hs[s][:, cols],
+                rhs=up[:, 2 * n * N_TILE : 2 * (n + 1) * N_TILE].bitcast(FP4X4),
+                rhs_scale=sc[:, 4, n_cols],
+                start=False,
+                stop=True,
+            )
+
+        def y_out(t, n):
+            dst = pv[t // 2][:, t % 2, n * N_TILE : (n + 1) * N_TILE]
+            nc.vector.tensor_tensor(out=dst, in0=yp[t, n][:], in1=dst, op=ADD)
+
+        yf = {}
+
+        def y_evac(t, n, eng="s"):
+            if n == 0:
+                yf[t] = xraw.tile([P, M], F32, name=f"xr0{t}")
+            dst = yf[t][:, n * N_TILE : (n + 1) * N_TILE]
+            if eng == "s":
+                nc.scalar.copy(out=dst, in_=yp[t, n][:])
+            else:
+                nc.vector.tensor_copy(out=dst, in_=yp[t, n][:])
+
+        def y_add(t):
+            dst = pv[t // 2][:, t % 2, :]
+            nc.vector.tensor_tensor(out=dst, in0=yf[t][:], in1=dst, op=ADD)
+
+        def x_split(s, g, cut):
+            w = SLICES[s][1]
+            new_xb(s, g)
+            cast_x(s, g, "s", 0, cut)
+            cast_x(s, g, "v", cut, w)
+
+        def y_w_all(t):
+            for n in (0, 1):
+                for g in range(GROUPS):
+                    y_w(t, n, g)
+
+        nc.vector.memset(sc[:].rearrange("p a n -> p (a n)").bitcast(I32), 0)
+        scale_loads = [(which, r) for which in range(3) for r in range(4)]
+        for g in range(GROUPS):
+            load_d(g)
+            load_scales(*scale_loads[2 * g])
+            load_scales(*scale_loads[2 * g + 1])
+        for g in range(GROUPS):
+            load_x(0, g)
+            load_scales(*scale_loads[8 + g])
+        load_w8(0)
+        load_w8(1)
+        load_w4()
+        load_x(1, 0)
+        load_x(1, 1)
+        load_up()
+        load_x(1, 2)
+        load_x(1, 3)
+        for g in range(GROUPS):
+            load_x(2, g)
+        for b in range(4):
+            load_prev(b)
+
+        for g in range(GROUPS):
+            new_db(g)
+            cast_d(g, "s", 0, 64)
+            cast_d(g, "v", 64, 128)
+            if g:
+                quant_d(g - 1)
+        for g in range(GROUPS):
+            x_split(0, g, 128)
+            quant_x(0, g)
+            if g == 0:
+                quant_d(3)
+            for j in range(PACK):
+                h_mm(0, j, g)
+        h_new(0)
+        for j in range(PACK):
+            h_evac(0, j, "svsv"[j])
+        for g in range(GROUPS):
+            for t in (0, 1):
+                for n in (0, 1):
+                    y_w(t, n, g)
+        h_inter(0, "v", 0, 256)
+        x_split(1, 0, 128)
+        h_quant(0)
+        x_split(1, 1, 128)
+        quant_x(1, 0)
+        quant_x(1, 1)
+        for t in (0, 1):
+            for n in (0, 1):
+                y_up(t, n)
+        x_split(1, 2, 128)
+        quant_x(1, 2)
+        y_evac(0, 0)
+        y_evac(0, 1)
+        x_split(1, 3, 128)
+        quant_x(1, 3)
+        y_evac(1, 0, "v")
+        for t in (2, 3):
+            for g in range(3):
+                for n in (0, 1):
+                    y_w(t, n, g)
+        for j in range(PACK):
+            for g in range(GROUPS):
+                h_mm(1, j, g)
+        for t in (2, 3):
+            for n in (0, 1):
+                y_w(t, n, 3)
+        h_new(1)
+        x_split(2, 0, 192)
+        y_evac(1, 1, "v")
+        quant_x(2, 0)
+        x_split(2, 1, 192)
+        h_evac(1, 0, "s")
+        h_evac(1, 2, "s")
+        quant_x(2, 1)
+        h_inter(1, "v", 0, 256)
+        h_quant(1)
+        for j in range(PACK):
+            h_mm(2, j, 0)
+        for j in range(PACK):
+            h_mm(2, j, 1)
+        for t in (2, 3):
+            for n in (0, 1):
+                y_up(t, n)
+        x_split(2, 2, 288)
+        y_evac(2, 0)
+        y_evac(2, 1)
+        quant_x(2, 2)
+        for j in range(PACK):
+            h_mm(2, j, 2)
+        x_split(2, 3, 192)
+        y_evac(3, 0)
+        y_evac(3, 1)
+        for n in (0, 1):
+            for g in range(3):
+                y_w(4, n, g)
+        quant_x(2, 3)
+        for j in range(PACK):
+            h_mm(2, j, 3)
+        h_new(2)
+        for j in range(PACK):
+            h_evac(2, j)
+        for n in (0, 1):
+            y_w(4, n, 3)
+        y_w_all(5)
+        for t in (0, 1, 2):
+            y_add(t)
+            store(t)
+        h_inter(2, "s", 0, 192)
+        h_inter(2, "v", 192, 512)
+        h_quant(2)
+        for g in range(GROUPS):
+            y_w(6, 0, g)
+        y_add(3)
+        store(3)
+        for t in (4, 5):
+            for n in (0, 1):
+                y_up(t, n)
+                y_out(t, n)
+            store(t)
+        for g in range(GROUPS):
+            y_w(6, 1, g)
+        for n in (0, 1):
+            y_up(6, n)
+            y_out(6, n)
+        store(6)
+        for n in (0, 1):
+            for g in range(GROUPS):
+                y_w(7, n, g)
+            y_up(7, n)
+            y_out(7, n)
+            store_half(7, n)

@@ -20,10 +20,8 @@ PACK = 4
 K_PASS = P * PACK
 N_TILE = 512
 GROUPS = K // K_PASS
-SLICES = ((0, 256), (256, 256), (512, 512))
-W_MAX = 512
-Y_BANKS = ("a0", "a1"), ("a2", "a3"), ("b0", "b1"), ("a0", "a1"), ("b0", "b1"), ("a0", "a1"), ("a2", "a3"), ("b2", "b3")
-H_BANKS = ("b0", "b1", "b2", "b3"), ("b2", "b2", "b3", "b3"), ("a2", "a3", "b2", "b3")
+HALF = 512
+CUT = 88
 
 
 def tile_mix_three_tm_res_kernel(
@@ -33,41 +31,54 @@ def tile_mix_three_tm_res_kernel(
     with ExitStack() as ctx:
         keep = ctx.enter_context(tc.tile_pool(name="keep", bufs=1))
         xraw = ctx.enter_context(tc.tile_pool(name="xraw", bufs=1))
-        draw = ctx.enter_context(tc.tile_pool(name="draw", bufs=4))
-        group = ctx.enter_context(tc.tile_pool(name="group", bufs=3))
-        hsb = ctx.enter_context(tc.tile_pool(name="hsb", bufs=1))
+        group = ctx.enter_context(tc.tile_pool(name="group", bufs=6))
         psum = ctx.enter_context(tc.psum_pool(name="psum", bufs=1))
         ctx.enter_context(tc.manual_schedule())
 
         w8 = keep.tile([P, 2, M], U32, name="w8", align_bytes=64)
         w4 = keep.tile([P, 2, 2 * M], U8, name="w4", align_bytes=64)
         up = keep.tile([P, 2 * M], U8, name="up", align_bytes=64)
-        sc = keep.tile([P, 5, M], U8, name="sc", align_bytes=64)
-        xq, xs, xr = {}, {}, {}
-        dq, ds, dr = {}, {}, {}
-        for s, (t0, w) in enumerate(SLICES):
-            for g in range(GROUPS):
-                xq[s, g] = keep.tile([P, w], U32, name=f"xq{s}{g}", align_bytes=64)
-                xs[s, g] = keep.tile([P, w], U8, name=f"xs{s}{g}", align_bytes=64)
+        s8 = keep.tile([P, 2, M], U8, name="s8", align_bytes=64)
+        s4 = keep.tile([P, 2, M], U8, name="s4", align_bytes=64)
+        su = keep.tile([P, 1, M], U8, name="su", align_bytes=64)
+        xq, xs, dq, ds, dr, hq, hs, hc = {}, {}, {}, {}, {}, {}, {}, {}
         for g in range(GROUPS):
+            for h in (0, 1):
+                xq[g, h] = keep.tile([P, HALF], U32, name=f"xq{g}{h}", align_bytes=64)
+                xs[g, h] = keep.tile([P, HALF], U8, name=f"xs{g}{h}", align_bytes=64)
             dq[g] = keep.tile([P, R], U32, name=f"dq{g}", align_bytes=64)
             ds[g] = keep.tile([P, R], U8, name=f"ds{g}", align_bytes=64)
-        pv = [keep.tile([P, 2, M], F32, name=f"pv{b}") for b in range(4)]
+            dr[g] = keep.tile([P, PACK * R], F32, name=f"dr{g}")
+        for h in (0, 1):
+            hq[h] = keep.tile([P, HALF], U32, name=f"hq{h}", align_bytes=64)
+            hs[h] = keep.tile([P, HALF], U8, name=f"hs{h}", align_bytes=64)
+            hc[h] = keep.tile([P, PACK * HALF], BF16, name=f"hc{h}")
+        pv = [keep.tile([P, 2 * M], F32, name=f"pv{b}") for b in range(4)]
+        prev_rows = prev.rearrange("(h p a) n -> h p (a n)", h=2, a=PACK)
+        out_rows = out.rearrange("(h p a) n -> h p (a n)", h=2, a=PACK)
 
-        def load_x(s, g):
-            t0, w = SLICES[s]
-            xr[s, g] = xraw.tile([P, PACK, w], F32, name=f"xr{s}{g}")
-            rows = x[g * K_PASS : (g + 1) * K_PASS, t0 : t0 + w]
-            nc.sync.dma_start(out=xr[s, g][:], in_=rows.rearrange("(p j) w -> p j w", j=PACK))
+        xsrc = {}
+
+        def load_x(g):
+            raw = xraw.tile([P, PACK * T], F32, name=f"xr{g}")
+            rows = x[g * K_PASS : (g + 1) * K_PASS, :]
+            nc.sync.dma_start(out=raw[:], in_=rows.rearrange("(p j) w -> p (j w)", j=PACK))
+            for h in (0, 1):
+                xsrc[g, h] = raw[:].rearrange("p (j h m a) -> p h m j a", j=PACK, h=2, a=PACK)[:, h]
+
+        def load_x_half(g, h):
+            raw = xraw.tile([P, PACK, HALF], F32, name=f"xr{g}{h}")
+            rows = x[g * K_PASS : (g + 1) * K_PASS, h * HALF : (h + 1) * HALF]
+            nc.sync.dma_start(out=raw[:], in_=rows.rearrange("(p j) w -> p j w", j=PACK))
+            xsrc[g, h] = raw[:].rearrange("p j (m a) -> p m j a", a=PACK)
 
         def load_d(g):
-            dr[g] = draw.tile([P, PACK, R], F32, name="dr")
             rows = down[g * K_PASS : (g + 1) * K_PASS, :]
-            nc.sync.dma_start(out=dr[g][:], in_=rows.rearrange("(p j) r -> p j r", j=PACK))
+            nc.sync.dma_start(out=dr[g][:], in_=rows.rearrange("(p j) r -> p (j r)", j=PACK))
 
-        def load_w8(a):
+        def load_w8():
             nc.sync.dma_start(
-                out=w8[:, a, :].bitcast(I32), in_=w8_words[a].rearrange("p n i -> p (n i)").bitcast(I32)
+                out=w8[:].bitcast(I32), in_=w8_words.rearrange("a p n i -> p a (n i)").bitcast(I32)
             )
 
         def load_w4():
@@ -76,319 +87,248 @@ def tile_mix_three_tm_res_kernel(
         def load_up():
             nc.sync.dma_start(out=up[:].bitcast(I32), in_=up_words[0].bitcast(I32))
 
-        def load_scales(which, r):
-            if which == 2:
-                dst = sc[r:P:32, 4, :]
-                src = up_scales[0].rearrange("(q r) n -> r q n", r=4)[r]
-            else:
-                scales = (w8_scales, w4_scales)[which]
-                dst = sc[r:P:32, 2 * which : 2 * which + 2, :]
-                src = scales.rearrange("a (q r) n -> r q a n", r=4)[r]
+        def load_scales(scales, planes, r):
+            dst = planes[r:P:32]
+            src = scales.rearrange("a (q r) n -> r q a n", r=4)[r]
             nc.sync.dma_start(out=dst.bitcast(I32), in_=src.bitcast(I32))
 
         def load_prev(b):
-            rows = prev[b * 256 : (b + 1) * 256, :]
-            nc.sync.dma_start(out=pv[b][:], in_=rows.rearrange("(a p) n -> p a n", p=P))
+            nc.sync.dma_start(out=pv[b][:], in_=prev_rows[b // 2][:, (b % 2) * 2 * M : (b % 2 + 1) * 2 * M])
 
-        def store(t):
-            nc.sync.dma_start(out=out[t * P : (t + 1) * P, :], in_=pv[t // 2][:, t % 2, :])
+        def res(t, c0, c1):
+            return pv[t // 2][:, (t % 2) * M + c0 : (t % 2) * M + c1]
 
-        def store_half(t, n):
-            n_cols = slice(n * N_TILE, (n + 1) * N_TILE)
-            nc.sync.dma_start(out=out[t * P : (t + 1) * P, n_cols], in_=pv[t // 2][:, t % 2, n_cols])
+        def store(t, c0=0, c1=M):
+            nc.sync.dma_start(out=out_rows[t // 4][:, (t % 4) * M + c0 : (t % 4) * M + c1], in_=res(t, c0, c1))
 
-        xb, db = {}, {}
-
-        def new_xb(s, g):
-            xb[s, g] = group.tile([P, PACK * W_MAX], BF16, name="xb", align_bytes=64)
-
-        def four(dst, src, c0, c1):
-            o = dst[:, PACK * c0 : PACK * c1].rearrange("p (c j) -> p c j", j=PACK)
-            i = src[:, :, c0:c1].rearrange("p j c -> p c j")
-            return o, i
-
-        def cast_x(s, g, eng, c0, c1):
-            o, i = four(xb[s, g], xr[s, g], c0, c1)
+        def copy(eng, dst, src):
             if eng == "v":
-                nc.vector.tensor_copy(out=o, in_=i)
+                nc.vector.tensor_copy(out=dst, in_=src)
             else:
-                nc.scalar.copy(out=o, in_=i)
+                nc.scalar.copy(out=dst, in_=src)
 
-        def quant_x(s, g):
-            w = SLICES[s][1]
-            parts = ((0, 128), (128, 256)) if w == 256 else ((0, w),)
-            for c0, c1 in parts:
-                nc.vector.quantize_mx(
-                    out=xq[s, g][:, c0:c1].bitcast(FP8X4),
-                    scales=xs[s, g][:, c0:c1],
-                    in_=xb[s, g][:, PACK * c0 : PACK * c1],
-                )
+        def cast(src, eng, dst, m0, m1):
+            o = dst[:].rearrange("p (a m j) -> p m j a", a=PACK, j=PACK)
+            copy(eng, o[:, m0:m1], src[:, m0:m1])
 
-        def new_db(g):
-            db[g] = group.tile([P, PACK * R], BF16, name="db", align_bytes=64)
+        def new_group():
+            grouped = group.tile([P, PACK * HALF], BF16, name="grouped", align_bytes=64)
+            return grouped
 
-        def cast_d(g, eng, m0, m1):
-            o = db[g][:].rearrange("p (t m j) -> p m t j", t=4, j=PACK)[:, m0:m1]
-            i = dr[g][:].rearrange("p j (m t) -> p m t j", t=4)[:, m0:m1]
-            if eng == "v":
-                nc.vector.tensor_copy(out=o, in_=i)
-            else:
-                nc.scalar.copy(out=o, in_=i)
+        def quant(codes, scales, src, c0=0, c1=HALF):
+            nc.vector.quantize_mx(
+                out=codes[:, c0:c1].bitcast(FP8X4), scales=scales[:, c0:c1], in_=src[:, PACK * c0 : PACK * c1]
+            )
 
-        def quant_d(g):
-            nc.vector.quantize_mx(out=dq[g][:].bitcast(FP8X4), scales=ds[g][:], in_=db[g][:])
+        def quant_halves(codes, scales, src):
+            quant(codes, scales, src, 0, HALF // 2)
+            quant(codes, scales, src, HALF // 2, HALF)
 
-        hp, hf, hb, hq, hs = {}, {}, {}, {}, {}
+        def dsrc(g):
+            return dr[g][:].rearrange("p (j m a) -> p m j a", j=PACK, a=PACK)
 
-        def h_mm(s, j, g):
-            w = SLICES[s][1]
-            shared = s == 1
-            if g == 0 and not (shared and j % 2):
-                hp[s, j] = psum.tile([P, W_MAX], F32, name=H_BANKS[s][j])
-                if shared:
-                    hp[s, j + 1] = hp[s, j]
-            c0 = w * (j % 2) if shared else 0
+        bank = {}
+
+        def new_bank(key, b):
+            bank[key] = psum.tile([P, N_TILE], F32, name=f"bank{b}")
+
+        def h_mm(h, j, g):
             cols = slice(j * P, (j + 1) * P)
             nc.tensor.matmul_mx(
-                out=hp[s, j][:, c0 : c0 + w],
+                out=bank["h", h, j][:],
                 lhsT=dq[g][:, cols].bitcast(FP8X4),
                 lhsT_scale=ds[g][:, cols],
-                rhs=xq[s, g][:].bitcast(FP8X4),
-                rhs_scale=xs[s, g][:],
+                rhs=xq[g, h][:].bitcast(FP8X4),
+                rhs_scale=xs[g, h][:],
                 start=(g == 0),
                 stop=(g == GROUPS - 1),
             )
 
-        def h_new(s):
-            w = SLICES[s][1]
-            hf[s] = hsb.tile([P, PACK, w], F32, name="hf")
-            hb[s] = hsb.tile([P, PACK * W_MAX], BF16, name="hb", align_bytes=64)
-            hq[s] = keep.tile([P, w], U32, name=f"hq{s}", align_bytes=64)
-            hs[s] = keep.tile([P, w], U8, name=f"hs{s}", align_bytes=64)
-
-        def h_evac(s, j, eng="s"):
-            w = SLICES[s][1]
-            if s == 1:
-                dst, src = hf[s][:, j : j + 2, :].rearrange("p j w -> p (j w)"), hp[s, j][:]
-            else:
-                dst, src = hf[s][:, j, :], hp[s, j][:, :w]
-            if eng == "s":
-                nc.scalar.copy(out=dst, in_=src)
-            else:
-                nc.vector.tensor_copy(out=dst, in_=src)
-
-        def h_inter(s, eng, c0, c1):
-            o, i = four(hb[s], hf[s], c0, c1)
-            if eng == "v":
-                nc.vector.tensor_copy(out=o, in_=i)
-            else:
-                nc.scalar.copy(out=o, in_=i)
-
-        def h_quant(s):
-            w = SLICES[s][1]
-            nc.vector.quantize_mx(out=hq[s][:].bitcast(FP8X4), scales=hs[s][:], in_=hb[s][:, : PACK * w])
-
-        yp = {}
-
-        def where(t):
-            for s, (t0, w) in enumerate(SLICES):
-                if t0 <= t * P < t0 + w:
-                    return s, t * P - t0
-
-        def y_w(t, n, g):
-            s, c = where(t)
-            cols = slice(c, c + P)
+        def y_w(t, n, g, stop=False):
+            cols = slice((t % 4) * P, (t % 4 + 1) * P)
             n_cols = slice(n * N_TILE, (n + 1) * N_TILE)
-            if g == 0:
-                yp[t, n] = psum.tile([P, N_TILE], F32, name=Y_BANKS[t][n])
             if g < 2:
                 rhs = w8[:, g, n_cols].bitcast(FP8X4)
             else:
                 rhs = w4[:, g - 2, 2 * n * N_TILE : 2 * (n + 1) * N_TILE].bitcast(FP4X4)
             nc.tensor.matmul_mx(
-                out=yp[t, n][:],
-                lhsT=xq[s, g][:, cols].bitcast(FP8X4),
-                lhsT_scale=xs[s, g][:, cols],
+                out=bank[t, n][:],
+                lhsT=xq[g, t // 4][:, cols].bitcast(FP8X4),
+                lhsT_scale=xs[g, t // 4][:, cols],
                 rhs=rhs,
-                rhs_scale=sc[:, g, n_cols],
+                rhs_scale=(s8, s4)[g // 2][:, g % 2, n_cols],
                 start=(g == 0),
-                stop=False,
+                stop=stop,
             )
 
-        def y_up(t, n):
-            s, c = where(t)
-            cols = slice(c, c + P)
+        def y_up(t, n, start=False):
+            cols = slice((t % 4) * P, (t % 4 + 1) * P)
             n_cols = slice(n * N_TILE, (n + 1) * N_TILE)
             nc.tensor.matmul_mx(
-                out=yp[t, n][:],
-                lhsT=hq[s][:, cols].bitcast(FP8X4),
-                lhsT_scale=hs[s][:, cols],
+                out=bank[t, n][:],
+                lhsT=hq[t // 4][:, cols].bitcast(FP8X4),
+                lhsT_scale=hs[t // 4][:, cols],
                 rhs=up[:, 2 * n * N_TILE : 2 * (n + 1) * N_TILE].bitcast(FP4X4),
-                rhs_scale=sc[:, 4, n_cols],
-                start=False,
+                rhs_scale=su[:, 0, n_cols],
+                start=start,
                 stop=True,
             )
 
-        def y_out(t, n):
-            dst = pv[t // 2][:, t % 2, n * N_TILE : (n + 1) * N_TILE]
-            nc.vector.tensor_tensor(out=dst, in0=yp[t, n][:], in1=dst, op=ADD)
-
-        yf = {}
-
-        def y_evac(t, n, eng="s"):
-            if n == 0:
-                yf[t] = xraw.tile([P, M], F32, name=f"xr0{t}")
-            dst = yf[t][:, n * N_TILE : (n + 1) * N_TILE]
-            if eng == "s":
-                nc.scalar.copy(out=dst, in_=yp[t, n][:])
-            else:
-                nc.vector.tensor_copy(out=dst, in_=yp[t, n][:])
-
-        def y_add(t):
-            dst = pv[t // 2][:, t % 2, :]
-            nc.vector.tensor_tensor(out=dst, in0=yf[t][:], in1=dst, op=ADD)
-
-        def x_split(s, g, cut):
-            w = SLICES[s][1]
-            new_xb(s, g)
-            cast_x(s, g, "s", 0, cut)
-            cast_x(s, g, "v", cut, w)
-
-        def y_w_all(t):
+        def y_w_all(t, b):
             for n in (0, 1):
+                new_bank((t, n), b + n)
                 for g in range(GROUPS):
                     y_w(t, n, g)
 
-        nc.vector.memset(sc[:].rearrange("p a n -> p (a n)").bitcast(I32), 0)
-        scale_loads = [(which, r) for which in range(3) for r in range(4)]
+        def y_up_alone(t, b):
+            for n in (0, 1):
+                new_bank((t, n), b + n)
+                y_up(t, n, start=True)
+
+        def y_out(t, n):
+            dst = res(t, n * N_TILE, (n + 1) * N_TILE)
+            nc.vector.tensor_tensor(out=dst, in0=bank[t, n][:], in1=dst, op=ADD)
+
+        def y_done(t):
+            y_out(t, 0)
+            y_out(t, 1)
+            store(t)
+
+        def interleave(eng, dst, h, c0, c1):
+            o = dst[:].rearrange("p (c i j) -> p c j i", i=4, j=PACK)
+            i = hc[h][:].rearrange("p (j c i) -> p c j i", i=4, j=PACK)
+            copy(eng, o[:, c0:c1], i[:, c0:c1])
+
+        def h_evac(eng, h, j):
+            copy(eng, hc[h][:, j * HALF : (j + 1) * HALF], bank["h", h, j][:])
+
+        load_x(0)
+        for planes in (s8, s4, su):
+            nc.vector.memset(planes[:].rearrange("p a n -> p (a n)").bitcast(I32), 0)
+        for r in range(4):
+            load_scales(w8_scales, s8, r)
+        load_x(1)
+        load_w8()
+        for r in range(2):
+            load_scales(w4_scales, s4, r)
+        load_x_half(2, 0)
+        for r in range(2, 4):
+            load_scales(w4_scales, s4, r)
+        load_w4()
+        load_x_half(3, 0)
         for g in range(GROUPS):
             load_d(g)
-            load_scales(*scale_loads[2 * g])
-            load_scales(*scale_loads[2 * g + 1])
-        for g in range(GROUPS):
-            load_x(0, g)
-            load_scales(*scale_loads[8 + g])
-        load_w8(0)
-        load_w8(1)
-        load_w4()
-        load_x(1, 0)
-        load_x(1, 1)
+        load_x_half(2, 1)
+        for r in range(2):
+            load_scales(up_scales, su, r)
         load_up()
-        load_x(1, 2)
-        load_x(1, 3)
-        for g in range(GROUPS):
-            load_x(2, g)
+        for r in range(2, 4):
+            load_scales(up_scales, su, r)
+        load_x_half(3, 1)
         for b in range(4):
             load_prev(b)
 
+        def shared(src, codes, scales, cut=CUT):
+            grouped = new_group()
+            cast(src, "v", grouped, 0, cut)
+            if cut < P:
+                cast(src, "s", grouped, cut, P)
+            quant_halves(codes, scales, grouped)
+
+        first = (2, 3, 1, 0)
+        for t in first:
+            for n in (0, 1):
+                new_bank((t, n), 2 * t + n)
         for g in range(GROUPS):
-            new_db(g)
-            cast_d(g, "s", 0, 64)
-            cast_d(g, "v", 64, 128)
-            if g:
-                quant_d(g - 1)
-        for g in range(GROUPS):
-            x_split(0, g, 128)
-            quant_x(0, g)
-            if g == 0:
-                quant_d(3)
+            for h in (0, 1) if g < 2 else (0,):
+                shared(xsrc[g, h], xq[g, h], xs[g, h])
+            for t in first:
+                for n in (0, 1):
+                    y_w(t, n, g, stop=(g == GROUPS - 1 and t > 0))
+
+        part = xraw.tile([P, PACK * M], F32, name="xr0")
+
+        def y_evac(eng, b):
+            copy(eng, part[:, b * N_TILE : (b + 1) * N_TILE], bank[b // 2, b % 2][:])
+
+        def y_add(t, c0=0, c1=M):
+            dst = res(t, c0, c1)
+            nc.vector.tensor_tensor(out=dst, in0=part[:, t * M + c0 : t * M + c1], in1=dst, op=ADD)
+
+        shared(dsrc(0), dq[0], ds[0], P)
+        for j in range(PACK):
+            y_evac("s", 4 + j)
+            new_bank(("h", 0, j), 4 + j)
+            h_mm(0, j, 0)
+        for j in (0, 1):
+            y_evac("s", 2 + j)
+            new_bank(("h", 1, j), 2 + j)
+            h_mm(1, j, 0)
+        for g in range(1, GROUPS):
+            shared(dsrc(g), dq[g], ds[g], P if g == 1 else CUT)
             for j in range(PACK):
                 h_mm(0, j, g)
-        h_new(0)
+            if g == 1:
+                for j in (0, 1):
+                    h_mm(1, j, g)
         for j in range(PACK):
-            h_evac(0, j, "svsv"[j])
-        for g in range(GROUPS):
-            for t in (0, 1):
-                for n in (0, 1):
-                    y_w(t, n, g)
-        h_inter(0, "v", 0, 256)
-        x_split(1, 0, 128)
-        h_quant(0)
-        x_split(1, 1, 128)
-        quant_x(1, 0)
-        quant_x(1, 1)
-        for t in (0, 1):
-            for n in (0, 1):
-                y_up(t, n)
-        x_split(1, 2, 128)
-        quant_x(1, 2)
-        y_evac(0, 0)
-        y_evac(0, 1)
-        x_split(1, 3, 128)
-        quant_x(1, 3)
-        y_evac(1, 0, "v")
-        for t in (2, 3):
-            for g in range(3):
-                for n in (0, 1):
-                    y_w(t, n, g)
-        for j in range(PACK):
-            for g in range(GROUPS):
+            h_evac("vsss"[j], 0, j)
+        shared(xsrc[2, 1], xq[2, 1], xs[2, 1], P)
+        for j in (2, 3):
+            new_bank(("h", 1, j), 2 + j)
+            for g in (0, 1):
                 h_mm(1, j, g)
-        for t in (2, 3):
-            for n in (0, 1):
-                y_w(t, n, 3)
-        h_new(1)
-        x_split(2, 0, 192)
-        y_evac(1, 1, "v")
-        quant_x(2, 0)
-        x_split(2, 1, 192)
-        h_evac(1, 0, "s")
-        h_evac(1, 2, "s")
-        quant_x(2, 1)
-        h_inter(1, "v", 0, 256)
-        h_quant(1)
-        for j in range(PACK):
-            h_mm(2, j, 0)
-        for j in range(PACK):
-            h_mm(2, j, 1)
-        for t in (2, 3):
-            for n in (0, 1):
-                y_up(t, n)
-        x_split(2, 2, 288)
-        y_evac(2, 0)
-        y_evac(2, 1)
-        quant_x(2, 2)
-        for j in range(PACK):
-            h_mm(2, j, 2)
-        x_split(2, 3, 192)
-        y_evac(3, 0)
-        y_evac(3, 1)
         for n in (0, 1):
-            for g in range(3):
+            new_bank((4, n), 6 + n)
+            for g in (0, 1):
                 y_w(4, n, g)
-        quant_x(2, 3)
         for j in range(PACK):
-            h_mm(2, j, 3)
-        h_new(2)
+            h_mm(1, j, 2)
+        for n in (0, 1):
+            y_w(4, n, 2)
+        hb = [new_group(), new_group()]
+        interleave("s", hb[0], 0, 80, P)
+        interleave("v", hb[0], 0, 0, 80)
+        quant(hq[0], hs[0], hb[0])
+        shared(xsrc[3, 1], xq[3, 1], xs[3, 1], 72)
+        for n in (0, 1):
+            y_up(0, n)
         for j in range(PACK):
-            h_evac(2, j)
+            h_mm(1, j, 3)
         for n in (0, 1):
             y_w(4, n, 3)
-        y_w_all(5)
-        for t in (0, 1, 2):
-            y_add(t)
-            store(t)
-        h_inter(2, "s", 0, 192)
-        h_inter(2, "v", 192, 512)
-        h_quant(2)
-        for g in range(GROUPS):
-            y_w(6, 0, g)
-        y_add(3)
-        store(3)
-        for t in (4, 5):
+        for j in range(PACK):
+            h_evac("s", 1, j)
+        y_done(0)
+        y_up_alone(1, 0)
+        for n in (0, 1):
+            new_bank((5, n), 2 + n)
+            for g in range(GROUPS):
+                y_w(5, n, g)
+            if n == 0:
+                y_up_alone(2, 4)
+        y_add(1)
+        y_done(1)
+        interleave("s", hb[1], 1, 0, P)
+        y_up_alone(3, 0)
+        y_add(2)
+        y_done(2)
+        y_w_all(6, 4)
+        y_add(3, 0, N_TILE)
+        quant(hq[1], hs[1], hb[1])
+        y_add(3, N_TILE, M)
+        for t in (4, 5, 6):
             for n in (0, 1):
                 y_up(t, n)
-                y_out(t, n)
-            store(t)
-        for g in range(GROUPS):
-            y_w(6, 1, g)
+        y_done(3)
+        y_done(4)
         for n in (0, 1):
-            y_up(6, n)
-            y_out(6, n)
-        store(6)
-        for n in (0, 1):
+            new_bank((7, n), 6 + n)
             for g in range(GROUPS):
                 y_w(7, n, g)
             y_up(7, n)
+        for t in (5, 6):
+            y_done(t)
+        for n in (0, 1):
             y_out(7, n)
-            store_half(7, n)
+            store(7, n * N_TILE, (n + 1) * N_TILE)

@@ -207,8 +207,8 @@ def tile_mix_three_tm_res_kernel(
             nc.vector.memset(planes[:].rearrange("p a n -> p (a n)").bitcast(I32), 0)
         for r in range(4):
             load_scales(w8_scales, s8, r)
-        load_x(1)
         load_w8()
+        load_x(1)
         for r in range(2):
             load_scales(w4_scales, s4, r)
         load_x_half(2, 0)
@@ -219,13 +219,13 @@ def tile_mix_three_tm_res_kernel(
         for g in range(GROUPS):
             load_d(g)
         load_x_half(2, 1)
+        load_x_half(3, 1)
         for r in range(2):
             load_scales(up_scales, su, r)
         load_up()
         for r in range(2, 4):
             load_scales(up_scales, su, r)
-        load_x_half(3, 1)
-        for b in range(4):
+        for b in (0, 2, 1, 3):
             load_prev(b)
 
         def shared(src, codes, scales, cut=CUT):
@@ -235,7 +235,7 @@ def tile_mix_three_tm_res_kernel(
                 cast(src, "s", grouped, cut, P)
             quant_halves(codes, scales, grouped)
 
-        first = (2, 3, 1, 0)
+        first = (2, 3, 0, 1)
         for t in first:
             for n in (0, 1):
                 new_bank((t, n), 2 * t + n)
@@ -244,7 +244,7 @@ def tile_mix_three_tm_res_kernel(
                 shared(xsrc[g, h], xq[g, h], xs[g, h])
             for t in first:
                 for n in (0, 1):
-                    y_w(t, n, g, stop=(g == GROUPS - 1 and t > 0))
+                    y_w(t, n, g, stop=(g == GROUPS - 1))
 
         part = xraw.tile([P, PACK * M], F32, name="xr0")
 
@@ -253,81 +253,74 @@ def tile_mix_three_tm_res_kernel(
 
         def y_add(t, c0=0, c1=M):
             dst = res(t, c0, c1)
-            nc.vector.tensor_tensor(out=dst, in0=part[:, t * M + c0 : t * M + c1], in1=dst, op=ADD)
+            (nc.vector if t < 2 else nc.gpsimd).tensor_tensor(out=dst, in0=part[:, t * M + c0 : t * M + c1], in1=dst, op=ADD)
 
         shared(dsrc(0), dq[0], ds[0], P)
-        for j in range(PACK):
-            y_evac("s", 4 + j)
-            new_bank(("h", 0, j), 4 + j)
-            h_mm(0, j, 0)
-        for j in (0, 1):
-            y_evac("s", 2 + j)
-            new_bank(("h", 1, j), 2 + j)
-            h_mm(1, j, 0)
-        for g in range(1, GROUPS):
-            shared(dsrc(g), dq[g], ds[g], P if g == 1 else CUT)
+        for h in (0, 1):
+            for j in range(PACK):
+                y_evac("s", 4 * (1 - h) + j)
+                new_bank(("h", h, j), 4 * (1 - h) + j)
+        second = [(j, g) for g in (0, 1) for j in range(PACK)]
+        for g, (i0, i1) in enumerate(((0, 2), (2, 6), (6, 8), (8, 8))):
+            if g:
+                shared(dsrc(g), dq[g], ds[g], P if g == 1 else CUT)
             for j in range(PACK):
                 h_mm(0, j, g)
-            if g == 1:
-                for j in (0, 1):
-                    h_mm(1, j, g)
+            for j, g1 in second[i0:i1]:
+                h_mm(1, j, g1)
         for j in range(PACK):
-            h_evac("vsss"[j], 0, j)
-        shared(xsrc[2, 1], xq[2, 1], xs[2, 1], P)
-        for j in (2, 3):
-            new_bank(("h", 1, j), 2 + j)
-            for g in (0, 1):
-                h_mm(1, j, g)
-        for n in (0, 1):
-            new_bank((4, n), 6 + n)
-            for g in (0, 1):
-                y_w(4, n, g)
-        for j in range(PACK):
-            h_mm(1, j, 2)
-        for n in (0, 1):
-            y_w(4, n, 2)
+            h_evac("s", 0, j)
+        xb = new_group()
+        cast(xsrc[2, 1], "v", xb, 0, P)
+        quant(xq[2, 1], xs[2, 1], xb)
+        for t in (4, 5):
+            for n in (0, 1):
+                new_bank((t, n), 2 * t - 4 + n)
+                for g in (0, 1):
+                    y_w(t, n, g)
         hb = [new_group(), new_group()]
-        interleave("s", hb[0], 0, 80, P)
-        interleave("v", hb[0], 0, 0, 80)
+        interleave("s", hb[0], 0, 0, P)
+        xb = new_group()
+        cast(xsrc[3, 1], "v", xb, 0, P)
+        quant(xq[3, 1], xs[3, 1], xb)
+        for g in (2, 3):
+            for j in range(PACK):
+                h_mm(1, j, g)
+            for t in (4, 5) if g == 2 else (4,):
+                for n in (0, 1):
+                    y_w(t, n, g)
         quant(hq[0], hs[0], hb[0])
-        shared(xsrc[3, 1], xq[3, 1], xs[3, 1], 72)
-        for n in (0, 1):
-            y_up(0, n)
-        for j in range(PACK):
-            h_mm(1, j, 3)
-        for n in (0, 1):
-            y_w(4, n, 3)
         for j in range(PACK):
             h_evac("s", 1, j)
-        y_done(0)
-        y_up_alone(1, 0)
+        y_up_alone(0, 0)
         for n in (0, 1):
-            new_bank((5, n), 2 + n)
-            for g in range(GROUPS):
-                y_w(5, n, g)
-            if n == 0:
-                y_up_alone(2, 4)
-        y_add(1)
-        y_done(1)
-        interleave("s", hb[1], 1, 0, P)
-        y_up_alone(3, 0)
-        y_add(2)
-        y_done(2)
-        y_w_all(6, 4)
-        y_add(3, 0, N_TILE)
+            y_w(5, n, 3)
+        y_up_alone(1, 2)
+        y_add(0)
+        y_add(1, 0, N_TILE)
+        y_done(0)
+        interleave("s", hb[1], 1, 64, P)
+        interleave("v", hb[1], 1, 0, 64)
+        y_add(1, N_TILE, M)
         quant(hq[1], hs[1], hb[1])
-        y_add(3, N_TILE, M)
+        for t in (2, 3):
+            for n in (0, 1):
+                y_add(t, n * N_TILE, (n + 1) * N_TILE)
+        y_w_all(6, 0)
         for t in (4, 5, 6):
             for n in (0, 1):
                 y_up(t, n)
-        y_done(3)
+        y_done(1)
+        y_up_alone(2, 2)
         y_done(4)
+        y_done(5)
+        y_up_alone(3, 6)
         for n in (0, 1):
-            new_bank((7, n), 6 + n)
+            new_bank((7, n), 4 + n)
             for g in range(GROUPS):
                 y_w(7, n, g)
             y_up(7, n)
-        for t in (5, 6):
+        for t in (2, 6, 3):
             y_done(t)
         for n in (0, 1):
             y_out(7, n)

@@ -220,12 +220,13 @@ def tile_mix_three_tm_res_kernel(
             load_d(g)
         load_x_half(2, 1)
         load_x_half(3, 1)
+        load_prev(0)
         for r in range(2):
             load_scales(up_scales, su, r)
         load_up()
         for r in range(2, 4):
             load_scales(up_scales, su, r)
-        for b in (0, 2, 1, 3):
+        for b in (1, 2, 3):
             load_prev(b)
 
         def shared(src, codes, scales, cut=CUT):
@@ -286,41 +287,44 @@ def tile_mix_three_tm_res_kernel(
         for g in (2, 3):
             for j in range(PACK):
                 h_mm(1, j, g)
-            for t in (4, 5) if g == 2 else (4,):
-                for n in (0, 1):
-                    y_w(t, n, g)
+            for n in (0, 1):
+                y_w(2 + g, n, 2)
+        y_add(0, 0, N_TILE)
         quant(hq[0], hs[0], hb[0])
         for j in range(PACK):
             h_evac("s", 1, j)
-        y_up_alone(0, 0)
-        for n in (0, 1):
-            y_w(5, n, 3)
-        y_up_alone(1, 2)
-        y_add(0)
-        y_add(1, 0, N_TILE)
-        y_done(0)
-        interleave("s", hb[1], 1, 64, P)
-        interleave("v", hb[1], 1, 0, 64)
-        y_add(1, N_TILE, M)
-        quant(hq[1], hs[1], hb[1])
+        interleave("s", hb[1], 1, 0, P)
+        for t in (0, 1):
+            y_up_alone(t, 2 * t)
+            for n in (0, 1):
+                y_w(4 + t, n, 3)
+        y_add(0, N_TILE, M)
+        y_add(1)
         for t in (2, 3):
             for n in (0, 1):
                 y_add(t, n * N_TILE, (n + 1) * N_TILE)
-        y_w_all(6, 0)
+        y_done(0)
+        y_up_alone(2, 0)
+        y_done(1)
+        for n in (0, 1):
+            new_bank((6, n), 2 + n)
+            for g in range(GROUPS):
+                y_w(6, n, g)
+            y_out(2, n)
+            new_bank((3, n), n)
+            y_up(3, n, start=True)
+        store(2)
+        quant(hq[1], hs[1], hb[1])
         for t in (4, 5, 6):
             for n in (0, 1):
                 y_up(t, n)
-        y_done(1)
-        y_up_alone(2, 2)
-        y_done(4)
-        y_done(5)
-        y_up_alone(3, 6)
+        y_done(3)
         for n in (0, 1):
-            new_bank((7, n), 4 + n)
+            new_bank((7, n), n)
             for g in range(GROUPS):
                 y_w(7, n, g)
             y_up(7, n)
-        for t in (2, 6, 3):
+        for t in (4, 5, 6):
             y_done(t)
         for n in (0, 1):
             y_out(7, n)

@@ -31,7 +31,7 @@ def tile_mix_three_tm_res_kernel(
     with ExitStack() as ctx:
         keep = ctx.enter_context(tc.tile_pool(name="keep", bufs=1))
         xraw = ctx.enter_context(tc.tile_pool(name="xraw", bufs=1))
-        group = ctx.enter_context(tc.tile_pool(name="group", bufs=6))
+        group = ctx.enter_context(tc.tile_pool(name="group", bufs=4))
         psum = ctx.enter_context(tc.psum_pool(name="psum", bufs=1))
         ctx.enter_context(tc.manual_schedule())
 
@@ -236,10 +236,10 @@ def tile_mix_three_tm_res_kernel(
                 cast(src, "s", grouped, cut, P)
             quant_halves(codes, scales, grouped)
 
-        first = (2, 3, 0, 1)
+        first = (0, 1, 2, 3)
         for t in first:
             for n in (0, 1):
-                new_bank((t, n), 2 * t + n)
+                new_bank((t, n), (2 * t + n + 4) % 8)
         for g in range(GROUPS):
             for h in (0, 1) if g < 2 else (0,):
                 shared(xsrc[g, h], xq[g, h], xs[g, h])
@@ -254,12 +254,12 @@ def tile_mix_three_tm_res_kernel(
 
         def y_add(t, c0=0, c1=M):
             dst = res(t, c0, c1)
-            (nc.vector if t < 2 else nc.gpsimd).tensor_tensor(out=dst, in0=part[:, t * M + c0 : t * M + c1], in1=dst, op=ADD)
+            nc.vector.tensor_tensor(out=dst, in0=part[:, t * M + c0 : t * M + c1], in1=dst, op=ADD)
 
         shared(dsrc(0), dq[0], ds[0], P)
         for h in (0, 1):
             for j in range(PACK):
-                y_evac("s", 4 * (1 - h) + j)
+                y_evac("s", 4 * h + j)
                 new_bank(("h", h, j), 4 * (1 - h) + j)
         second = [(j, g) for g in (0, 1) for j in range(PACK)]
         for g, (i0, i1) in enumerate(((0, 2), (2, 6), (6, 8), (8, 8))):
@@ -279,7 +279,7 @@ def tile_mix_three_tm_res_kernel(
                 new_bank((t, n), 2 * t - 4 + n)
                 for g in (0, 1):
                     y_w(t, n, g)
-        hb = [new_group(), new_group()]
+        hb = [keep.tile([P, PACK * HALF], BF16, name=f"hb{h}", align_bytes=64) for h in (0, 1)]
         interleave("s", hb[0], 0, 0, P)
         xb = new_group()
         cast(xsrc[3, 1], "v", xb, 0, P)
@@ -300,32 +300,52 @@ def tile_mix_three_tm_res_kernel(
                 y_w(4 + t, n, 3)
         y_add(0, N_TILE, M)
         y_add(1)
-        for t in (2, 3):
+        def y_add_pool(t, base):
             for n in (0, 1):
-                y_add(t, n * N_TILE, (n + 1) * N_TILE)
+                c0, c1 = n * N_TILE, (n + 1) * N_TILE
+                nc.gpsimd.tensor_tensor(
+                    out=base[:, c0:c1], in0=part[:, t * M + c0 : t * M + c1], in1=res(t, c0, c1), op=ADD
+                )
+
+        def y_out_from(t, n, base):
+            c0, c1 = n * N_TILE, (n + 1) * N_TILE
+            nc.vector.tensor_tensor(out=res(t, c0, c1), in0=bank[t, n][:], in1=base[:, c0:c1], op=ADD)
+
+        base2 = part[:, M : 2 * M]
+        y_add_pool(2, base2)
         y_done(0)
         y_up_alone(2, 0)
         y_done(1)
+        y_out_from(2, 0, base2)
+        quant(hq[1], hs[1], hb[1])
+        y_out_from(2, 1, base2)
+        store(2)
+        base3 = keep.tile([P, M], F32, name="hb1", align_bytes=64)
+        y_add_pool(3, base3)
         for n in (0, 1):
             new_bank((6, n), 2 + n)
-            for g in range(GROUPS):
-                y_w(6, n, g)
-            y_out(2, n)
-            new_bank((3, n), n)
-            y_up(3, n, start=True)
-        store(2)
-        quant(hq[1], hs[1], hb[1])
-        for t in (4, 5, 6):
+        six = [(n, g) for n in (0, 1) for g in range(GROUPS)]
+        for n, g in six[:6]:
+            y_w(6, n, g)
+        for t in (4, 5):
             for n in (0, 1):
                 y_up(t, n)
-        y_done(3)
+        for n, g in six[6:]:
+            y_w(6, n, g)
+        for n in (0, 1):
+            y_up(6, n)
+        y_done(4)
+        y_up_alone(3, 4)
         for n in (0, 1):
             new_bank((7, n), n)
             for g in range(GROUPS):
                 y_w(7, n, g)
             y_up(7, n)
-        for t in (4, 5, 6):
-            y_done(t)
+        y_done(5)
+        y_done(6)
+        for n in (0, 1):
+            y_out_from(3, n, base3)
+        store(3)
         for n in (0, 1):
             y_out(7, n)
             store(7, n * N_TILE, (n + 1) * N_TILE)

@@ -53,7 +53,9 @@ def tile_mix_three_tm_res_kernel(
             hq[h] = keep.tile([P, HALF], U32, name=f"hq{h}", align_bytes=64)
             hs[h] = keep.tile([P, HALF], U8, name=f"hs{h}", align_bytes=64)
             hc[h] = keep.tile([P, PACK * HALF], BF16, name=f"hc{h}")
-        pv = [keep.tile([P, 2 * M], F32, name=f"pv{b}") for b in range(4)]
+        pv = [keep.tile([P, 2 * M], F32, name=f"pv{b}") for b in range(2)]
+        second_half = keep.tile([P, 4 * M], F32, name="pv2")
+        pv.extend([second_half[:, : 2 * M], second_half[:, 2 * M :]])
         prev_rows = prev.rearrange("(h p a) n -> h p (a n)", h=2, a=PACK)
         out_rows = out.rearrange("(h p a) n -> h p (a n)", h=2, a=PACK)
 
@@ -189,10 +191,11 @@ def tile_mix_three_tm_res_kernel(
             dst = res(t, n * N_TILE, (n + 1) * N_TILE)
             nc.vector.tensor_tensor(out=dst, in0=bank[t, n][:], in1=dst, op=ADD)
 
-        def y_done(t):
+        def y_done(t, tiles=1):
             y_out(t, 0)
             y_out(t, 1)
-            store(t)
+            if tiles:
+                store(t + 1 - tiles, 0, tiles * M)
 
         def interleave(eng, dst, h, c0, c1):
             o = dst[:].rearrange("p (c i j) -> p c j i", i=4, j=PACK)
@@ -226,8 +229,8 @@ def tile_mix_three_tm_res_kernel(
         load_up()
         for r in range(2, 4):
             load_scales(up_scales, su, r)
-        for b in (1, 2, 3):
-            load_prev(b)
+        load_prev(1)
+        nc.sync.dma_start(out=second_half[:], in_=prev_rows[1])
 
         def shared(src, codes, scales, cut=CUT):
             grouped = new_group()
@@ -293,7 +296,8 @@ def tile_mix_three_tm_res_kernel(
         quant(hq[0], hs[0], hb[0])
         for j in range(PACK):
             h_evac("s", 1, j)
-        interleave("s", hb[1], 1, 0, P)
+        interleave("s", hb[1], 1, 0, P // 2)
+        interleave("s", hb[1], 1, P // 2, P)
         for t in (0, 1):
             y_up_alone(t, 2 * t)
             for n in (0, 1):
@@ -313,13 +317,14 @@ def tile_mix_three_tm_res_kernel(
 
         base2 = part[:, M : 2 * M]
         y_add_pool(2, base2)
-        y_done(0)
+        y_done(0, 0)
         y_up_alone(2, 0)
-        y_done(1)
+        y_done(1, 2)
         y_out_from(2, 0, base2)
-        quant(hq[1], hs[1], hb[1])
+        quant(hq[1], hs[1], hb[1], 0, HALF // 2)
         y_out_from(2, 1, base2)
         store(2)
+        quant(hq[1], hs[1], hb[1], HALF // 2, HALF)
         base3 = keep.tile([P, M], F32, name="hb1", align_bytes=64)
         y_add_pool(3, base3)
         for n in (0, 1):

@@ -35,12 +35,12 @@ def tile_mix_three_tm_res_kernel(
         psum = ctx.enter_context(tc.psum_pool(name="psum", bufs=1))
         ctx.enter_context(tc.manual_schedule())
 
-        w8 = keep.tile([P, 2, M], U32, name="w8", align_bytes=64)
-        w4 = keep.tile([P, 2, 2 * M], U8, name="w4", align_bytes=64)
-        up = keep.tile([P, 2 * M], U8, name="up", align_bytes=64)
-        s8 = keep.tile([P, 2, M], U8, name="s8", align_bytes=64)
-        s4 = keep.tile([P, 2, M], U8, name="s4", align_bytes=64)
-        su = keep.tile([P, 1, M], U8, name="su", align_bytes=64)
+        w8 = keep.tile([P, 2, M], U32, name="w8", align_bytes=256)
+        w4 = keep.tile([P, 2, 2 * M], U8, name="w4", align_bytes=256)
+        up = keep.tile([P, 2 * M], U8, name="up", align_bytes=256)
+        s8 = keep.tile([P, 2, M], U8, name="s8", align_bytes=256)
+        s4 = keep.tile([P, 2, M], U8, name="s4", align_bytes=256)
+        su = keep.tile([P, 1, M], U8, name="su", align_bytes=256)
         xq, xs, dq, ds, dr, hq, hs, hc = {}, {}, {}, {}, {}, {}, {}, {}
         for g in range(GROUPS):
             for h in (0, 1):
@@ -48,13 +48,13 @@ def tile_mix_three_tm_res_kernel(
                 xs[g, h] = keep.tile([P, HALF], U8, name=f"xs{g}{h}", align_bytes=64)
             dq[g] = keep.tile([P, R], U32, name=f"dq{g}", align_bytes=64)
             ds[g] = keep.tile([P, R], U8, name=f"ds{g}", align_bytes=64)
-            dr[g] = keep.tile([P, PACK * R], F32, name=f"dr{g}")
+            dr[g] = keep.tile([P, PACK * R], F32, name=f"dr{g}", align_bytes=256)
         for h in (0, 1):
             hq[h] = keep.tile([P, HALF], U32, name=f"hq{h}", align_bytes=64)
             hs[h] = keep.tile([P, HALF], U8, name=f"hs{h}", align_bytes=64)
             hc[h] = keep.tile([P, PACK * HALF], BF16, name=f"hc{h}")
-        pv = [keep.tile([P, 2 * M], F32, name=f"pv{b}") for b in range(2)]
-        second_half = keep.tile([P, 4 * M], F32, name="pv2")
+        pv = [keep.tile([P, 2 * M], F32, name=f"pv{b}", align_bytes=256) for b in range(2)]
+        second_half = keep.tile([P, 4 * M], F32, name="pv2", align_bytes=256)
         pv.extend([second_half[:, : 2 * M], second_half[:, 2 * M :]])
         prev_rows = prev.rearrange("(h p a) n -> h p (a n)", h=2, a=PACK)
         out_rows = out.rearrange("(h p a) n -> h p (a n)", h=2, a=PACK)
@@ -62,14 +62,14 @@ def tile_mix_three_tm_res_kernel(
         xsrc = {}
 
         def load_x(g):
-            raw = xraw.tile([P, PACK * T], F32, name=f"xr{g}")
+            raw = xraw.tile([P, PACK * T], F32, name=f"xr{g}", align_bytes=256)
             rows = x[g * K_PASS : (g + 1) * K_PASS, :]
             nc.sync.dma_start(out=raw[:], in_=rows.rearrange("(p j) w -> p (j w)", j=PACK))
             for h in (0, 1):
                 xsrc[g, h] = raw[:].rearrange("p (j h m a) -> p h m j a", j=PACK, h=2, a=PACK)[:, h]
 
         def load_x_half(g, h):
-            raw = xraw.tile([P, PACK, HALF], F32, name=f"xr{g}{h}")
+            raw = xraw.tile([P, PACK, HALF], F32, name=f"xr{g}{h}", align_bytes=256)
             rows = x[g * K_PASS : (g + 1) * K_PASS, h * HALF : (h + 1) * HALF]
             nc.sync.dma_start(out=raw[:], in_=rows.rearrange("(p j) w -> p j w", j=PACK))
             xsrc[g, h] = raw[:].rearrange("p j (m a) -> p m j a", a=PACK)
@@ -250,7 +250,7 @@ def tile_mix_three_tm_res_kernel(
                 for n in (0, 1):
                     y_w(t, n, g, stop=(g == GROUPS - 1))
 
-        part = xraw.tile([P, PACK * M], F32, name="xr0")
+        part = xraw.tile([P, PACK * M], F32, name="xr0", align_bytes=256)
 
         def y_evac(eng, b):
             copy(eng, part[:, b * N_TILE : (b + 1) * N_TILE], bank[b // 2, b % 2][:])

@@ -20,8 +20,16 @@ PACK = 4
 K_PASS = P * PACK
 N_TILE = 512
 GROUPS = K // K_PASS
-HALF = 512
-CUT = 88
+W8_GROUPS = O // K_PASS
+HALF = T // 2
+HALF_TILES = HALF // P
+BANKS = 8
+DMA_ALIGN = 256
+MX_ALIGN = 64
+STAGING_BUFS = 4
+VECTOR_SHARE = 88
+SECOND_H_PASSES = (2, 4, 2, 0)
+TILE6_LEAD = 6
 
 
 def tile_mix_three_tm_res_kernel(
@@ -31,326 +39,296 @@ def tile_mix_three_tm_res_kernel(
     with ExitStack() as ctx:
         keep = ctx.enter_context(tc.tile_pool(name="keep", bufs=1))
         xraw = ctx.enter_context(tc.tile_pool(name="xraw", bufs=1))
-        group = ctx.enter_context(tc.tile_pool(name="group", bufs=4))
+        staging = ctx.enter_context(tc.tile_pool(name="group", bufs=STAGING_BUFS))
         psum = ctx.enter_context(tc.psum_pool(name="psum", bufs=1))
         ctx.enter_context(tc.manual_schedule())
 
-        w8 = keep.tile([P, 2, M], U32, name="w8", align_bytes=256)
-        w4 = keep.tile([P, 2, 2 * M], U8, name="w4", align_bytes=256)
-        up = keep.tile([P, 2 * M], U8, name="up", align_bytes=256)
-        s8 = keep.tile([P, 2, M], U8, name="s8", align_bytes=256)
-        s4 = keep.tile([P, 2, M], U8, name="s4", align_bytes=256)
-        su = keep.tile([P, 1, M], U8, name="su", align_bytes=256)
-        xq, xs, dq, ds, dr, hq, hs, hc = {}, {}, {}, {}, {}, {}, {}, {}
+        w8 = keep.tile([P, 2, M], U32, name="w8", align_bytes=DMA_ALIGN)
+        w4 = keep.tile([P, 2, 2 * M], U8, name="w4", align_bytes=DMA_ALIGN)
+        up = keep.tile([P, 2 * M], U8, name="up", align_bytes=DMA_ALIGN)
+        w8_planes = keep.tile([P, 2, M], U8, name="s8", align_bytes=DMA_ALIGN)
+        w4_planes = keep.tile([P, 2, M], U8, name="s4", align_bytes=DMA_ALIGN)
+        up_planes = keep.tile([P, 1, M], U8, name="su", align_bytes=DMA_ALIGN)
+        x_codes, x_plane, d_codes, d_plane, d_raw, h_codes, h_plane, h_split = {}, {}, {}, {}, {}, {}, {}, {}
         for g in range(GROUPS):
             for h in (0, 1):
-                xq[g, h] = keep.tile([P, HALF], U32, name=f"xq{g}{h}", align_bytes=64)
-                xs[g, h] = keep.tile([P, HALF], U8, name=f"xs{g}{h}", align_bytes=64)
-            dq[g] = keep.tile([P, R], U32, name=f"dq{g}", align_bytes=64)
-            ds[g] = keep.tile([P, R], U8, name=f"ds{g}", align_bytes=64)
-            dr[g] = keep.tile([P, PACK * R], F32, name=f"dr{g}", align_bytes=256)
+                x_codes[g, h] = keep.tile([P, HALF], U32, name=f"xq{g}{h}", align_bytes=MX_ALIGN)
+                x_plane[g, h] = keep.tile([P, HALF], U8, name=f"xs{g}{h}", align_bytes=MX_ALIGN)
+            d_codes[g] = keep.tile([P, R], U32, name=f"dq{g}", align_bytes=MX_ALIGN)
+            d_plane[g] = keep.tile([P, R], U8, name=f"ds{g}", align_bytes=MX_ALIGN)
+            d_raw[g] = keep.tile([P, PACK * R], F32, name=f"dr{g}", align_bytes=DMA_ALIGN)
         for h in (0, 1):
-            hq[h] = keep.tile([P, HALF], U32, name=f"hq{h}", align_bytes=64)
-            hs[h] = keep.tile([P, HALF], U8, name=f"hs{h}", align_bytes=64)
-            hc[h] = keep.tile([P, PACK * HALF], BF16, name=f"hc{h}")
-        pv = [keep.tile([P, 2 * M], F32, name=f"pv{b}", align_bytes=256) for b in range(2)]
-        second_half = keep.tile([P, 4 * M], F32, name="pv2", align_bytes=256)
-        pv.extend([second_half[:, : 2 * M], second_half[:, 2 * M :]])
-        prev_rows = prev.rearrange("(h p a) n -> h p (a n)", h=2, a=PACK)
-        out_rows = out.rearrange("(h p a) n -> h p (a n)", h=2, a=PACK)
+            h_codes[h] = keep.tile([P, HALF], U32, name=f"hq{h}", align_bytes=MX_ALIGN)
+            h_plane[h] = keep.tile([P, HALF], U8, name=f"hs{h}", align_bytes=MX_ALIGN)
+            h_split[h] = keep.tile([P, PACK * HALF], BF16, name=f"hc{h}")
+        pair = [keep.tile([P, 2 * M], F32, name=f"pv{b}", align_bytes=DMA_ALIGN) for b in range(2)]
+        second_half = keep.tile([P, HALF_TILES * M], F32, name="pv2", align_bytes=DMA_ALIGN)
+        pair.extend([second_half[:, : 2 * M], second_half[:, 2 * M :]])
+        prev_rows = prev.rearrange("(h p a) n -> h p (a n)", h=2, a=HALF_TILES)
+        out_rows = out.rearrange("(h p a) n -> h p (a n)", h=2, a=HALF_TILES)
 
-        xsrc = {}
+        x_view = {}
 
-        def load_x(g):
-            raw = xraw.tile([P, PACK * T], F32, name=f"xr{g}", align_bytes=256)
+        def load_x_whole(g):
+            raw = xraw.tile([P, PACK * T], F32, name=f"xr{g}", align_bytes=DMA_ALIGN)
             rows = x[g * K_PASS : (g + 1) * K_PASS, :]
             nc.sync.dma_start(out=raw[:], in_=rows.rearrange("(p j) w -> p (j w)", j=PACK))
             for h in (0, 1):
-                xsrc[g, h] = raw[:].rearrange("p (j h m a) -> p h m j a", j=PACK, h=2, a=PACK)[:, h]
+                x_view[g, h] = raw[:].rearrange("p (j h m a) -> p h m j a", j=PACK, h=2, a=HALF_TILES)[:, h]
 
         def load_x_half(g, h):
-            raw = xraw.tile([P, PACK, HALF], F32, name=f"xr{g}{h}", align_bytes=256)
+            raw = xraw.tile([P, PACK, HALF], F32, name=f"xr{g}{h}", align_bytes=DMA_ALIGN)
             rows = x[g * K_PASS : (g + 1) * K_PASS, h * HALF : (h + 1) * HALF]
             nc.sync.dma_start(out=raw[:], in_=rows.rearrange("(p j) w -> p j w", j=PACK))
-            xsrc[g, h] = raw[:].rearrange("p j (m a) -> p m j a", a=PACK)
+            x_view[g, h] = raw[:].rearrange("p j (m a) -> p m j a", a=HALF_TILES)
 
-        def load_d(g):
+        def load_down(g):
             rows = down[g * K_PASS : (g + 1) * K_PASS, :]
-            nc.sync.dma_start(out=dr[g][:], in_=rows.rearrange("(p j) r -> p (j r)", j=PACK))
+            nc.sync.dma_start(out=d_raw[g][:], in_=rows.rearrange("(p j) r -> p (j r)", j=PACK))
 
-        def load_w8():
-            nc.sync.dma_start(
-                out=w8[:].bitcast(I32), in_=w8_words.rearrange("a p n i -> p a (n i)").bitcast(I32)
-            )
+        def load_scales(scales, planes, rows):
+            for r in rows:
+                src = scales.rearrange("a (q r) n -> r q a n", r=4)[r]
+                nc.sync.dma_start(out=planes[r:P:32].bitcast(I32), in_=src.bitcast(I32))
 
-        def load_w4():
-            nc.sync.dma_start(out=w4[:].bitcast(I32), in_=w4_words.rearrange("a p n -> p a n").bitcast(I32))
+        def load_prev_pair(b):
+            nc.sync.dma_start(out=pair[b][:], in_=prev_rows[0][:, b * 2 * M : (b + 1) * 2 * M])
 
-        def load_up():
-            nc.sync.dma_start(out=up[:].bitcast(I32), in_=up_words[0].bitcast(I32))
-
-        def load_scales(scales, planes, r):
-            dst = planes[r:P:32]
-            src = scales.rearrange("a (q r) n -> r q a n", r=4)[r]
-            nc.sync.dma_start(out=dst.bitcast(I32), in_=src.bitcast(I32))
-
-        def load_prev(b):
-            nc.sync.dma_start(out=pv[b][:], in_=prev_rows[b // 2][:, (b % 2) * 2 * M : (b % 2 + 1) * 2 * M])
-
-        def res(t, c0, c1):
-            return pv[t // 2][:, (t % 2) * M + c0 : (t % 2) * M + c1]
+        def result(t, c0, c1):
+            return pair[t // 2][:, (t % 2) * M + c0 : (t % 2) * M + c1]
 
         def store(t, c0=0, c1=M):
-            nc.sync.dma_start(out=out_rows[t // 4][:, (t % 4) * M + c0 : (t % 4) * M + c1], in_=res(t, c0, c1))
+            first = (t % HALF_TILES) * M
+            nc.sync.dma_start(out=out_rows[t // HALF_TILES][:, first + c0 : first + c1], in_=result(t, c0, c1))
 
-        def copy(eng, dst, src):
-            if eng == "v":
-                nc.vector.tensor_copy(out=dst, in_=src)
-            else:
-                nc.scalar.copy(out=dst, in_=src)
+        def new_staged():
+            staged = staging.tile([P, PACK * HALF], BF16, name="grouped", align_bytes=MX_ALIGN)
+            return staged
 
-        def cast(src, eng, dst, m0, m1):
-            o = dst[:].rearrange("p (a m j) -> p m j a", a=PACK, j=PACK)
-            copy(eng, o[:, m0:m1], src[:, m0:m1])
+        def staged_view(staged):
+            return staged[:].rearrange("p (a m j) -> p m j a", a=HALF_TILES, j=PACK)
 
-        def new_group():
-            grouped = group.tile([P, PACK * HALF], BF16, name="grouped", align_bytes=64)
-            return grouped
-
-        def quant(codes, scales, src, c0=0, c1=HALF):
+        def quantise(codes, plane, src, c0=0, c1=HALF):
             nc.vector.quantize_mx(
-                out=codes[:, c0:c1].bitcast(FP8X4), scales=scales[:, c0:c1], in_=src[:, PACK * c0 : PACK * c1]
+                out=codes[:, c0:c1].bitcast(FP8X4), scales=plane[:, c0:c1], in_=src[:, PACK * c0 : PACK * c1]
             )
 
-        def quant_halves(codes, scales, src):
-            quant(codes, scales, src, 0, HALF // 2)
-            quant(codes, scales, src, HALF // 2, HALF)
+        def round_and_quantise(src, codes, plane, share):
+            staged = new_staged()
+            nc.vector.tensor_copy(out=staged_view(staged)[:, :share], in_=src[:, :share])
+            if share < P:
+                nc.scalar.copy(out=staged_view(staged)[:, share:], in_=src[:, share:])
+            quantise(codes, plane, staged, 0, HALF // 2)
+            quantise(codes, plane, staged, HALF // 2, HALF)
 
-        def dsrc(g):
-            return dr[g][:].rearrange("p (j m a) -> p m j a", j=PACK, a=PACK)
+        def round_and_quantise_second_half(g):
+            staged = new_staged()
+            nc.vector.tensor_copy(out=staged_view(staged), in_=x_view[g, 1])
+            quantise(x_codes[g, 1], x_plane[g, 1], staged)
+
+        def down_view(g):
+            return d_raw[g][:].rearrange("p (j m a) -> p m j a", j=PACK, a=PACK)
 
         bank = {}
 
         def new_bank(key, b):
             bank[key] = psum.tile([P, N_TILE], F32, name=f"bank{b}")
 
-        def h_mm(h, j, g):
+        def h_pass(h, j, g):
             cols = slice(j * P, (j + 1) * P)
             nc.tensor.matmul_mx(
                 out=bank["h", h, j][:],
-                lhsT=dq[g][:, cols].bitcast(FP8X4),
-                lhsT_scale=ds[g][:, cols],
-                rhs=xq[g, h][:].bitcast(FP8X4),
-                rhs_scale=xs[g, h][:],
+                lhsT=d_codes[g][:, cols].bitcast(FP8X4),
+                lhsT_scale=d_plane[g][:, cols],
+                rhs=x_codes[g, h][:].bitcast(FP8X4),
+                rhs_scale=x_plane[g, h][:],
                 start=(g == 0),
                 stop=(g == GROUPS - 1),
             )
 
-        def y_w(t, n, g, stop=False):
-            cols = slice((t % 4) * P, (t % 4 + 1) * P)
+        def weight_pass(t, n, g, stop=False):
+            cols = slice((t % HALF_TILES) * P, (t % HALF_TILES + 1) * P)
             n_cols = slice(n * N_TILE, (n + 1) * N_TILE)
-            if g < 2:
+            if g < W8_GROUPS:
                 rhs = w8[:, g, n_cols].bitcast(FP8X4)
+                rhs_scale = w8_planes[:, g, n_cols]
             else:
-                rhs = w4[:, g - 2, 2 * n * N_TILE : 2 * (n + 1) * N_TILE].bitcast(FP4X4)
+                rhs = w4[:, g - W8_GROUPS, 2 * n * N_TILE : 2 * (n + 1) * N_TILE].bitcast(FP4X4)
+                rhs_scale = w4_planes[:, g - W8_GROUPS, n_cols]
             nc.tensor.matmul_mx(
                 out=bank[t, n][:],
-                lhsT=xq[g, t // 4][:, cols].bitcast(FP8X4),
-                lhsT_scale=xs[g, t // 4][:, cols],
+                lhsT=x_codes[g, t // HALF_TILES][:, cols].bitcast(FP8X4),
+                lhsT_scale=x_plane[g, t // HALF_TILES][:, cols],
                 rhs=rhs,
-                rhs_scale=(s8, s4)[g // 2][:, g % 2, n_cols],
+                rhs_scale=rhs_scale,
                 start=(g == 0),
                 stop=stop,
             )
 
-        def y_up(t, n, start=False):
-            cols = slice((t % 4) * P, (t % 4 + 1) * P)
-            n_cols = slice(n * N_TILE, (n + 1) * N_TILE)
+        def up_pass(t, n, start=False):
+            cols = slice((t % HALF_TILES) * P, (t % HALF_TILES + 1) * P)
             nc.tensor.matmul_mx(
                 out=bank[t, n][:],
-                lhsT=hq[t // 4][:, cols].bitcast(FP8X4),
-                lhsT_scale=hs[t // 4][:, cols],
+                lhsT=h_codes[t // HALF_TILES][:, cols].bitcast(FP8X4),
+                lhsT_scale=h_plane[t // HALF_TILES][:, cols],
                 rhs=up[:, 2 * n * N_TILE : 2 * (n + 1) * N_TILE].bitcast(FP4X4),
-                rhs_scale=su[:, 0, n_cols],
+                rhs_scale=up_planes[:, 0, n * N_TILE : (n + 1) * N_TILE],
                 start=start,
                 stop=True,
             )
 
-        def y_w_all(t, b):
+        def up_alone(t, b):
             for n in (0, 1):
                 new_bank((t, n), b + n)
-                for g in range(GROUPS):
-                    y_w(t, n, g)
+                up_pass(t, n, start=True)
 
-        def y_up_alone(t, b):
-            for n in (0, 1):
-                new_bank((t, n), b + n)
-                y_up(t, n, start=True)
-
-        def y_out(t, n):
-            dst = res(t, n * N_TILE, (n + 1) * N_TILE)
-            nc.vector.tensor_tensor(out=dst, in0=bank[t, n][:], in1=dst, op=ADD)
-
-        def y_done(t, tiles=1):
-            y_out(t, 0)
-            y_out(t, 1)
-            if tiles:
-                store(t + 1 - tiles, 0, tiles * M)
-
-        def interleave(eng, dst, h, c0, c1):
-            o = dst[:].rearrange("p (c i j) -> p c j i", i=4, j=PACK)
-            i = hc[h][:].rearrange("p (j c i) -> p c j i", i=4, j=PACK)
-            copy(eng, o[:, c0:c1], i[:, c0:c1])
-
-        def h_evac(eng, h, j):
-            copy(eng, hc[h][:, j * HALF : (j + 1) * HALF], bank["h", h, j][:])
-
-        load_x(0)
-        for planes in (s8, s4, su):
-            nc.vector.memset(planes[:].rearrange("p a n -> p (a n)").bitcast(I32), 0)
-        for r in range(4):
-            load_scales(w8_scales, s8, r)
-        load_w8()
-        load_x(1)
-        for r in range(2):
-            load_scales(w4_scales, s4, r)
-        load_x_half(2, 0)
-        for r in range(2, 4):
-            load_scales(w4_scales, s4, r)
-        load_w4()
-        load_x_half(3, 0)
-        for g in range(GROUPS):
-            load_d(g)
-        load_x_half(2, 1)
-        load_x_half(3, 1)
-        load_prev(0)
-        for r in range(2):
-            load_scales(up_scales, su, r)
-        load_up()
-        for r in range(2, 4):
-            load_scales(up_scales, su, r)
-        load_prev(1)
-        nc.sync.dma_start(out=second_half[:], in_=prev_rows[1])
-
-        def shared(src, codes, scales, cut=CUT):
-            grouped = new_group()
-            cast(src, "v", grouped, 0, cut)
-            if cut < P:
-                cast(src, "s", grouped, cut, P)
-            quant_halves(codes, scales, grouped)
-
-        first = (0, 1, 2, 3)
-        for t in first:
-            for n in (0, 1):
-                new_bank((t, n), (2 * t + n + 4) % 8)
-        for g in range(GROUPS):
-            for h in (0, 1) if g < 2 else (0,):
-                shared(xsrc[g, h], xq[g, h], xs[g, h])
-            for t in first:
-                for n in (0, 1):
-                    y_w(t, n, g, stop=(g == GROUPS - 1))
-
-        part = xraw.tile([P, PACK * M], F32, name="xr0", align_bytes=256)
-
-        def y_evac(eng, b):
-            copy(eng, part[:, b * N_TILE : (b + 1) * N_TILE], bank[b // 2, b % 2][:])
-
-        def y_add(t, c0=0, c1=M):
-            dst = res(t, c0, c1)
-            nc.vector.tensor_tensor(out=dst, in0=part[:, t * M + c0 : t * M + c1], in1=dst, op=ADD)
-
-        shared(dsrc(0), dq[0], ds[0], P)
-        for h in (0, 1):
+        def h_out(h):
             for j in range(PACK):
-                y_evac("s", 4 * h + j)
-                new_bank(("h", h, j), 4 * (1 - h) + j)
-        second = [(j, g) for g in (0, 1) for j in range(PACK)]
-        for g, (i0, i1) in enumerate(((0, 2), (2, 6), (6, 8), (8, 8))):
-            if g:
-                shared(dsrc(g), dq[g], ds[g], P if g == 1 else CUT)
-            for j in range(PACK):
-                h_mm(0, j, g)
-            for j, g1 in second[i0:i1]:
-                h_mm(1, j, g1)
-        for j in range(PACK):
-            h_evac("s", 0, j)
-        xb = new_group()
-        cast(xsrc[2, 1], "v", xb, 0, P)
-        quant(xq[2, 1], xs[2, 1], xb)
-        for t in (4, 5):
+                nc.scalar.copy(out=h_split[h][:, j * HALF : (j + 1) * HALF], in_=bank["h", h, j][:])
+
+        def h_interleave(h, c0, c1):
+            dst = h_words[h][:].rearrange("p (c i j) -> p c j i", i=4, j=PACK)
+            src = h_split[h][:].rearrange("p (j c i) -> p c j i", i=4, j=PACK)
+            nc.scalar.copy(out=dst[:, c0:c1], in_=src[:, c0:c1])
+
+        def add_bank(t, n, base):
+            c0, c1 = n * N_TILE, (n + 1) * N_TILE
+            nc.vector.tensor_tensor(out=result(t, c0, c1), in0=bank[t, n][:], in1=base[:, c0:c1], op=ADD)
+
+        def add_banks(t, base):
             for n in (0, 1):
-                new_bank((t, n), 2 * t - 4 + n)
-                for g in (0, 1):
-                    y_w(t, n, g)
-        hb = [keep.tile([P, PACK * HALF], BF16, name=f"hb{h}", align_bytes=64) for h in (0, 1)]
-        interleave("s", hb[0], 0, 0, P)
-        xb = new_group()
-        cast(xsrc[3, 1], "v", xb, 0, P)
-        quant(xq[3, 1], xs[3, 1], xb)
-        for g in (2, 3):
-            for j in range(PACK):
-                h_mm(1, j, g)
-            for n in (0, 1):
-                y_w(2 + g, n, 2)
-        y_add(0, 0, N_TILE)
-        quant(hq[0], hs[0], hb[0])
-        for j in range(PACK):
-            h_evac("s", 1, j)
-        interleave("s", hb[1], 1, 0, P // 2)
-        interleave("s", hb[1], 1, P // 2, P)
-        for t in (0, 1):
-            y_up_alone(t, 2 * t)
-            for n in (0, 1):
-                y_w(4 + t, n, 3)
-        y_add(0, N_TILE, M)
-        y_add(1)
-        def y_add_pool(t, base):
+                add_bank(t, n, base)
+
+        def add_partial(t, c0=0, c1=M):
+            dst = result(t, c0, c1)
+            nc.vector.tensor_tensor(out=dst, in0=partial[:, t * M + c0 : t * M + c1], in1=dst, op=ADD)
+
+        def add_partial_on_gpsimd(t, base):
             for n in (0, 1):
                 c0, c1 = n * N_TILE, (n + 1) * N_TILE
                 nc.gpsimd.tensor_tensor(
-                    out=base[:, c0:c1], in0=part[:, t * M + c0 : t * M + c1], in1=res(t, c0, c1), op=ADD
+                    out=base[:, c0:c1], in0=partial[:, t * M + c0 : t * M + c1], in1=result(t, c0, c1), op=ADD
                 )
 
-        def y_out_from(t, n, base):
-            c0, c1 = n * N_TILE, (n + 1) * N_TILE
-            nc.vector.tensor_tensor(out=res(t, c0, c1), in0=bank[t, n][:], in1=base[:, c0:c1], op=ADD)
+        load_x_whole(0)
+        for planes in (w8_planes, w4_planes, up_planes):
+            nc.vector.memset(planes[:].rearrange("p a n -> p (a n)").bitcast(I32), 0)
+        load_scales(w8_scales, w8_planes, (0, 1))
+        nc.sync.dma_start(out=w8[:].bitcast(I32), in_=w8_words.rearrange("a p n i -> p a (n i)").bitcast(I32))
+        load_scales(w8_scales, w8_planes, (2, 3))
+        load_x_whole(1)
+        load_scales(w4_scales, w4_planes, (0,))
+        nc.sync.dma_start(out=w4[:].bitcast(I32), in_=w4_words.rearrange("a p n -> p a n").bitcast(I32))
+        load_scales(w4_scales, w4_planes, (1,))
+        load_x_half(2, 0)
+        load_scales(w4_scales, w4_planes, (2, 3))
+        load_x_half(3, 0)
+        for g in range(GROUPS):
+            load_down(g)
+        load_x_half(2, 1)
+        load_scales(up_scales, up_planes, (0,))
+        load_x_half(3, 1)
+        load_scales(up_scales, up_planes, (1,))
+        load_prev_pair(0)
+        load_scales(up_scales, up_planes, (2,))
+        nc.sync.dma_start(out=up[:].bitcast(I32), in_=up_words[0].bitcast(I32))
+        load_scales(up_scales, up_planes, (3,))
+        load_prev_pair(1)
+        nc.sync.dma_start(out=second_half[:], in_=prev_rows[1])
 
-        base2 = part[:, M : 2 * M]
-        y_add_pool(2, base2)
-        y_done(0, 0)
-        y_up_alone(2, 0)
-        y_done(1, 2)
-        y_out_from(2, 0, base2)
-        quant(hq[1], hs[1], hb[1], 0, HALF // 2)
-        y_out_from(2, 1, base2)
-        store(2)
-        quant(hq[1], hs[1], hb[1], HALF // 2, HALF)
-        base3 = keep.tile([P, M], F32, name="hb1", align_bytes=64)
-        y_add_pool(3, base3)
-        for n in (0, 1):
-            new_bank((6, n), 2 + n)
-        six = [(n, g) for n in (0, 1) for g in range(GROUPS)]
-        for n, g in six[:6]:
-            y_w(6, n, g)
+        for t in range(HALF_TILES):
+            for n in (0, 1):
+                new_bank((t, n), (2 * t + n + BANKS // 2) % BANKS)
+        for g in range(GROUPS):
+            for h in (0, 1) if g < W8_GROUPS else (0,):
+                round_and_quantise(x_view[g, h], x_codes[g, h], x_plane[g, h], VECTOR_SHARE)
+            for t in range(HALF_TILES):
+                for n in (0, 1):
+                    weight_pass(t, n, g, stop=(g == GROUPS - 1))
+
+        partial = xraw.tile([P, HALF_TILES * M], F32, name="xr0", align_bytes=DMA_ALIGN)
+        round_and_quantise(down_view(0), d_codes[0], d_plane[0], P)
+        for h in (0, 1):
+            for j in range(PACK):
+                b = PACK * h + j
+                nc.scalar.copy(out=partial[:, b * N_TILE : (b + 1) * N_TILE], in_=bank[b // 2, b % 2][:])
+                new_bank(("h", h, j), PACK * (1 - h) + j)
+        second_h = [(j, g) for g in range(W8_GROUPS) for j in range(PACK)]
+        for g in range(GROUPS):
+            if g:
+                round_and_quantise(down_view(g), d_codes[g], d_plane[g], P if g == 1 else VECTOR_SHARE)
+            for j in range(PACK):
+                h_pass(0, j, g)
+            done = sum(SECOND_H_PASSES[:g])
+            for j, early in second_h[done : done + SECOND_H_PASSES[g]]:
+                h_pass(1, j, early)
+
+        h_out(0)
+        round_and_quantise_second_half(2)
         for t in (4, 5):
             for n in (0, 1):
-                y_up(t, n)
-        for n, g in six[6:]:
-            y_w(6, n, g)
+                new_bank((t, n), 2 * t - 4 + n)
+                for g in range(W8_GROUPS):
+                    weight_pass(t, n, g)
+        h_words = [keep.tile([P, PACK * HALF], BF16, name=f"hb{h}", align_bytes=MX_ALIGN) for h in (0, 1)]
+        h_interleave(0, 0, P)
+        round_and_quantise_second_half(3)
+        for g, t in ((2, 4), (3, 5)):
+            for j in range(PACK):
+                h_pass(1, j, g)
+            for n in (0, 1):
+                weight_pass(t, n, 2)
+        add_partial(0, 0, N_TILE)
+        quantise(h_codes[0], h_plane[0], h_words[0])
+        h_out(1)
+        h_interleave(1, 0, P // 2)
+        h_interleave(1, P // 2, P)
+
+        for t in (0, 1):
+            up_alone(t, 2 * t)
+            for n in (0, 1):
+                weight_pass(HALF_TILES + t, n, 3)
+        add_partial(0, N_TILE, M)
+        add_partial(1)
+        base2 = partial[:, M : 2 * M]
+        add_partial_on_gpsimd(2, base2)
+        add_banks(0, result(0, 0, M))
+        up_alone(2, 0)
+        add_banks(1, result(1, 0, M))
+        store(0, 0, 2 * M)
+        add_bank(2, 0, base2)
+        quantise(h_codes[1], h_plane[1], h_words[1], 0, HALF // 2)
+        add_bank(2, 1, base2)
+        store(2)
+        quantise(h_codes[1], h_plane[1], h_words[1], HALF // 2, HALF)
+        base3 = keep.tile([P, M], F32, name="hb1", align_bytes=MX_ALIGN)
+        add_partial_on_gpsimd(3, base3)
+
         for n in (0, 1):
-            y_up(6, n)
-        y_done(4)
-        y_up_alone(3, 4)
+            new_bank((6, n), 2 + n)
+        tile6 = [(n, g) for n in (0, 1) for g in range(GROUPS)]
+        for n, g in tile6[:TILE6_LEAD]:
+            weight_pass(6, n, g)
+        for t in (4, 5):
+            for n in (0, 1):
+                up_pass(t, n)
+        for n, g in tile6[TILE6_LEAD:]:
+            weight_pass(6, n, g)
+        for n in (0, 1):
+            up_pass(6, n)
+        add_banks(4, result(4, 0, M))
+        store(4)
+        up_alone(3, 4)
         for n in (0, 1):
             new_bank((7, n), n)
             for g in range(GROUPS):
-                y_w(7, n, g)
-            y_up(7, n)
-        y_done(5)
-        y_done(6)
-        for n in (0, 1):
-            y_out_from(3, n, base3)
+                weight_pass(7, n, g)
+            up_pass(7, n)
+        for t in (5, 6):
+            add_banks(t, result(t, 0, M))
+            store(t)
+        add_banks(3, base3)
         store(3)
         for n in (0, 1):
-            y_out(7, n)
+            add_bank(7, n, result(7, 0, M))
             store(7, n * N_TILE, (n + 1) * N_TILE)

@@ -225,14 +225,11 @@ def tile_mix_three_tm_res_kernel(
         load_x_half(3, 0)
         for g in range(GROUPS):
             load_down(g)
+            load_scales(up_scales, up_planes, (g,))
         load_x_half(2, 1)
-        load_scales(up_scales, up_planes, (0,))
         load_x_half(3, 1)
-        load_scales(up_scales, up_planes, (1,))
         load_prev_pair(0)
-        load_scales(up_scales, up_planes, (2,))
         nc.sync.dma_start(out=up[:].bitcast(I32), in_=up_words[0].bitcast(I32))
-        load_scales(up_scales, up_planes, (3,))
         load_prev_pair(1)
         nc.sync.dma_start(out=second_half[:], in_=prev_rows[1])
 

from contextlib import ExitStack

import concourse.mybir as mybir

O, K, R, M, T = 1024, 2048, 512, 1024, 1024
FLOPS = 2 * T * (K * R + K * M + R * M)
BYTES = 4 * (K * T + K * R + 2 * T * M) + O * M + (K - O) * M // 2 + R * M // 2 + (K + R) * M // 32

F32 = mybir.dt.float32
BF16 = mybir.dt.bfloat16
U32 = mybir.dt.uint32
I32 = mybir.dt.int32
U8 = mybir.dt.uint8
FP8X4 = mybir.dt.float8_e4m3fn_x4
FP4X4 = mybir.dt.float4_e2m1fn_x4
ADD = mybir.AluOpType.add

P = 128
PACK = 4
K_PASS = P * PACK
N_TILE = 512
GROUPS = K // K_PASS
W8_GROUPS = O // K_PASS
HALF = T // 2
HALF_TILES = HALF // P
BANKS = 8
DMA_ALIGN = 256
MX_ALIGN = 64
STAGING_BUFS = 4
VECTOR_SHARE = 88
SECOND_H_PASSES = (2, 4, 2, 0)
TILE6_LEAD = 6


def tile_mix_three_tm_res_kernel(
    tc, x, w8_words, w8_scales, w4_words, w4_scales, down, up_words, up_scales, prev, out
):
    nc = tc.nc
    with ExitStack() as ctx:
        keep = ctx.enter_context(tc.tile_pool(name="keep", bufs=1))
        xraw = ctx.enter_context(tc.tile_pool(name="xraw", bufs=1))
        staging = ctx.enter_context(tc.tile_pool(name="group", bufs=STAGING_BUFS))
        psum = ctx.enter_context(tc.psum_pool(name="psum", bufs=1))
        ctx.enter_context(tc.manual_schedule())

        w8 = keep.tile([P, 2, M], U32, name="w8", align_bytes=DMA_ALIGN)
        w4 = keep.tile([P, 2, 2 * M], U8, name="w4", align_bytes=DMA_ALIGN)
        up = keep.tile([P, 2 * M], U8, name="up", align_bytes=DMA_ALIGN)
        w8_planes = keep.tile([P, 2, M], U8, name="s8", align_bytes=DMA_ALIGN)
        w4_planes = keep.tile([P, 2, M], U8, name="s4", align_bytes=DMA_ALIGN)
        up_planes = keep.tile([P, 1, M], U8, name="su", align_bytes=DMA_ALIGN)
        x_codes, x_plane, d_codes, d_plane, d_raw, h_codes, h_plane, h_split = {}, {}, {}, {}, {}, {}, {}, {}
        for g in range(GROUPS):
            for h in (0, 1):
                x_codes[g, h] = keep.tile([P, HALF], U32, name=f"xq{g}{h}", align_bytes=MX_ALIGN)
                x_plane[g, h] = keep.tile([P, HALF], U8, name=f"xs{g}{h}", align_bytes=MX_ALIGN)
            d_codes[g] = keep.tile([P, R], U32, name=f"dq{g}", align_bytes=MX_ALIGN)
            d_plane[g] = keep.tile([P, R], U8, name=f"ds{g}", align_bytes=MX_ALIGN)
            d_raw[g] = keep.tile([P, PACK * R], F32, name=f"dr{g}", align_bytes=DMA_ALIGN)
        for h in (0, 1):
            h_codes[h] = keep.tile([P, HALF], U32, name=f"hq{h}", align_bytes=MX_ALIGN)
            h_plane[h] = keep.tile([P, HALF], U8, name=f"hs{h}", align_bytes=MX_ALIGN)
            h_split[h] = keep.tile([P, PACK * HALF], BF16, name=f"hc{h}")
        pair = [keep.tile([P, 2 * M], F32, name=f"pv{b}", align_bytes=DMA_ALIGN) for b in range(2)]
        second_half = keep.tile([P, HALF_TILES * M], F32, name="pv2", align_bytes=DMA_ALIGN)
        pair.extend([second_half[:, : 2 * M], second_half[:, 2 * M :]])
        prev_rows = prev.rearrange("(h p a) n -> h p (a n)", h=2, a=HALF_TILES)
        out_rows = out.rearrange("(h p a) n -> h p (a n)", h=2, a=HALF_TILES)

        x_view = {}

        def load_x_whole(g):
            raw = xraw.tile([P, PACK * T], F32, name=f"xr{g}", align_bytes=DMA_ALIGN)
            rows = x[g * K_PASS : (g + 1) * K_PASS, :]
            nc.sync.dma_start(out=raw[:], in_=rows.rearrange("(p j) w -> p (j w)", j=PACK))
            for h in (0, 1):
                x_view[g, h] = raw[:].rearrange("p (j h m a) -> p h m j a", j=PACK, h=2, a=HALF_TILES)[:, h]

        def load_x_half(g, h):
            raw = xraw.tile([P, PACK, HALF], F32, name=f"xr{g}{h}", align_bytes=DMA_ALIGN)
            rows = x[g * K_PASS : (g + 1) * K_PASS, h * HALF : (h + 1) * HALF]
            nc.sync.dma_start(out=raw[:], in_=rows.rearrange("(p j) w -> p j w", j=PACK))
            x_view[g, h] = raw[:].rearrange("p j (m a) -> p m j a", a=HALF_TILES)

        def load_down(g):
            rows = down[g * K_PASS : (g + 1) * K_PASS, :]
            nc.sync.dma_start(out=d_raw[g][:], in_=rows.rearrange("(p j) r -> p (j r)", j=PACK))

        def load_scales(scales, planes, rows):
            for r in rows:
                src = scales.rearrange("a (q r) n -> r q a n", r=4)[r]
                nc.sync.dma_start(out=planes[r:P:32].bitcast(I32), in_=src.bitcast(I32))

        def load_prev_pair(b):
            nc.sync.dma_start(out=pair[b][:], in_=prev_rows[0][:, b * 2 * M : (b + 1) * 2 * M])

        def result(t, c0, c1):
            return pair[t // 2][:, (t % 2) * M + c0 : (t % 2) * M + c1]

        def store(t, c0=0, c1=M):
            first = (t % HALF_TILES) * M
            nc.sync.dma_start(out=out_rows[t // HALF_TILES][:, first + c0 : first + c1], in_=result(t, c0, c1))

        def new_staged():
            staged = staging.tile([P, PACK * HALF], BF16, name="grouped", align_bytes=MX_ALIGN)
            return staged

        def staged_view(staged):
            return staged[:].rearrange("p (a m j) -> p m j a", a=HALF_TILES, j=PACK)

        def quantise(codes, plane, src, c0=0, c1=HALF):
            nc.vector.quantize_mx(
                out=codes[:, c0:c1].bitcast(FP8X4), scales=plane[:, c0:c1], in_=src[:, PACK * c0 : PACK * c1]
            )

        def round_and_quantise(src, codes, plane, share):
            staged = new_staged()
            nc.vector.tensor_copy(out=staged_view(staged)[:, :share], in_=src[:, :share])
            if share < P:
                nc.scalar.copy(out=staged_view(staged)[:, share:], in_=src[:, share:])
            quantise(codes, plane, staged, 0, HALF // 2)
            quantise(codes, plane, staged, HALF // 2, HALF)

        def round_and_quantise_second_half(g):
            staged = new_staged()
            nc.vector.tensor_copy(out=staged_view(staged), in_=x_view[g, 1])
            quantise(x_codes[g, 1], x_plane[g, 1], staged)

        def down_view(g):
            return d_raw[g][:].rearrange("p (j m a) -> p m j a", j=PACK, a=PACK)

        bank = {}

        def new_bank(key, b):
            bank[key] = psum.tile([P, N_TILE], F32, name=f"bank{b}")

        def h_pass(h, j, g):
            cols = slice(j * P, (j + 1) * P)
            nc.tensor.matmul_mx(
                out=bank["h", h, j][:],
                lhsT=d_codes[g][:, cols].bitcast(FP8X4),
                lhsT_scale=d_plane[g][:, cols],
                rhs=x_codes[g, h][:].bitcast(FP8X4),
                rhs_scale=x_plane[g, h][:],
                start=(g == 0),
                stop=(g == GROUPS - 1),
            )

        def weight_pass(t, n, g, stop=False):
            cols = slice((t % HALF_TILES) * P, (t % HALF_TILES + 1) * P)
            n_cols = slice(n * N_TILE, (n + 1) * N_TILE)
            if g < W8_GROUPS:
                rhs = w8[:, g, n_cols].bitcast(FP8X4)
                rhs_scale = w8_planes[:, g, n_cols]
            else:
                rhs = w4[:, g - W8_GROUPS, 2 * n * N_TILE : 2 * (n + 1) * N_TILE].bitcast(FP4X4)
                rhs_scale = w4_planes[:, g - W8_GROUPS, n_cols]
            nc.tensor.matmul_mx(
                out=bank[t, n][:],
                lhsT=x_codes[g, t // HALF_TILES][:, cols].bitcast(FP8X4),
                lhsT_scale=x_plane[g, t // HALF_TILES][:, cols],
                rhs=rhs,
                rhs_scale=rhs_scale,
                start=(g == 0),
                stop=stop,
            )

        def up_pass(t, n, start=False):
            cols = slice((t % HALF_TILES) * P, (t % HALF_TILES + 1) * P)
            nc.tensor.matmul_mx(
                out=bank[t, n][:],
                lhsT=h_codes[t // HALF_TILES][:, cols].bitcast(FP8X4),
                lhsT_scale=h_plane[t // HALF_TILES][:, cols],
                rhs=up[:, 2 * n * N_TILE : 2 * (n + 1) * N_TILE].bitcast(FP4X4),
                rhs_scale=up_planes[:, 0, n * N_TILE : (n + 1) * N_TILE],
                start=start,
                stop=True,
            )

        def up_alone(t, b):
            for n in (0, 1):
                new_bank((t, n), b + n)
                up_pass(t, n, start=True)

        def h_out(h):
            for j in range(PACK):
                nc.scalar.copy(out=h_split[h][:, j * HALF : (j + 1) * HALF], in_=bank["h", h, j][:])

        def h_interleave(h, c0, c1):
            dst = h_words[h][:].rearrange("p (c i j) -> p c j i", i=4, j=PACK)
            src = h_split[h][:].rearrange("p (j c i) -> p c j i", i=4, j=PACK)
            nc.scalar.copy(out=dst[:, c0:c1], in_=src[:, c0:c1])

        def add_bank(t, n, base):
            c0, c1 = n * N_TILE, (n + 1) * N_TILE
            nc.vector.tensor_tensor(out=result(t, c0, c1), in0=bank[t, n][:], in1=base[:, c0:c1], op=ADD)

        def add_banks(t, base):
            for n in (0, 1):
                add_bank(t, n, base)

        def add_partial(t, c0=0, c1=M):
            dst = result(t, c0, c1)
            nc.vector.tensor_tensor(out=dst, in0=partial[:, t * M + c0 : t * M + c1], in1=dst, op=ADD)

        def add_partial_on_gpsimd(t, base):
            for n in (0, 1):
                c0, c1 = n * N_TILE, (n + 1) * N_TILE
                nc.gpsimd.tensor_tensor(
                    out=base[:, c0:c1], in0=partial[:, t * M + c0 : t * M + c1], in1=result(t, c0, c1), op=ADD
                )

        load_x_whole(0)
        for planes in (w8_planes, w4_planes, up_planes):
            nc.vector.memset(planes[:].rearrange("p a n -> p (a n)").bitcast(I32), 0)
        load_scales(w8_scales, w8_planes, (0, 1))
        nc.sync.dma_start(out=w8[:].bitcast(I32), in_=w8_words.rearrange("a p n i -> p a (n i)").bitcast(I32))
        load_scales(w8_scales, w8_planes, (2, 3))
        load_x_whole(1)
        load_scales(w4_scales, w4_planes, (0,))
        nc.sync.dma_start(out=w4[:].bitcast(I32), in_=w4_words.rearrange("a p n -> p a n").bitcast(I32))
        load_scales(w4_scales, w4_planes, (1,))
        load_x_half(2, 0)
        load_scales(w4_scales, w4_planes, (2, 3))
        load_x_half(3, 0)
        for g in range(GROUPS):
            load_down(g)
            load_scales(up_scales, up_planes, (g,))
        load_x_half(2, 1)
        load_x_half(3, 1)
        load_prev_pair(0)
        nc.sync.dma_start(out=up[:].bitcast(I32), in_=up_words[0].bitcast(I32))
        load_prev_pair(1)
        nc.sync.dma_start(out=second_half[:], in_=prev_rows[1])

        for t in range(HALF_TILES):
            for n in (0, 1):
                new_bank((t, n), (2 * t + n + BANKS // 2) % BANKS)
        for g in range(GROUPS):
            for h in (0, 1) if g < W8_GROUPS else (0,):
                round_and_quantise(x_view[g, h], x_codes[g, h], x_plane[g, h], VECTOR_SHARE)
            for t in range(HALF_TILES):
                for n in (0, 1):
                    weight_pass(t, n, g, stop=(g == GROUPS - 1))

        partial = xraw.tile([P, HALF_TILES * M], F32, name="xr0", align_bytes=DMA_ALIGN)
        round_and_quantise(down_view(0), d_codes[0], d_plane[0], P)
        for h in (0, 1):
            for j in range(PACK):
                b = PACK * h + j
                nc.scalar.copy(out=partial[:, b * N_TILE : (b + 1) * N_TILE], in_=bank[b // 2, b % 2][:])
                new_bank(("h", h, j), PACK * (1 - h) + j)
        second_h = [(j, g) for g in range(W8_GROUPS) for j in range(PACK)]
        for g in range(GROUPS):
            if g:
                round_and_quantise(down_view(g), d_codes[g], d_plane[g], P if g == 1 else VECTOR_SHARE)
            for j in range(PACK):
                h_pass(0, j, g)
            done = sum(SECOND_H_PASSES[:g])
            for j, early in second_h[done : done + SECOND_H_PASSES[g]]:
                h_pass(1, j, early)

        h_out(0)
        round_and_quantise_second_half(2)
        for t in (4, 5):
            for n in (0, 1):
                new_bank((t, n), 2 * t - 4 + n)
                for g in range(W8_GROUPS):
                    weight_pass(t, n, g)
        h_words = [keep.tile([P, PACK * HALF], BF16, name=f"hb{h}", align_bytes=MX_ALIGN) for h in (0, 1)]
        h_interleave(0, 0, P)
        round_and_quantise_second_half(3)
        for g, t in ((2, 4), (3, 5)):
            for j in range(PACK):
                h_pass(1, j, g)
            for n in (0, 1):
                weight_pass(t, n, 2)
        add_partial(0, 0, N_TILE)
        quantise(h_codes[0], h_plane[0], h_words[0])
        h_out(1)
        h_interleave(1, 0, P // 2)
        h_interleave(1, P // 2, P)

        for t in (0, 1):
            up_alone(t, 2 * t)
            for n in (0, 1):
                weight_pass(HALF_TILES + t, n, 3)
        add_partial(0, N_TILE, M)
        add_partial(1)
        base2 = partial[:, M : 2 * M]
        add_partial_on_gpsimd(2, base2)
        add_banks(0, result(0, 0, M))
        up_alone(2, 0)
        add_banks(1, result(1, 0, M))
        store(0, 0, 2 * M)
        add_bank(2, 0, base2)
        quantise(h_codes[1], h_plane[1], h_words[1], 0, HALF // 2)
        add_bank(2, 1, base2)
        store(2)
        quantise(h_codes[1], h_plane[1], h_words[1], HALF // 2, HALF)
        base3 = keep.tile([P, M], F32, name="hb1", align_bytes=MX_ALIGN)
        add_partial_on_gpsimd(3, base3)

        for n in (0, 1):
            new_bank((6, n), 2 + n)
        tile6 = [(n, g) for n in (0, 1) for g in range(GROUPS)]
        for n, g in tile6[:TILE6_LEAD]:
            weight_pass(6, n, g)
        for t in (4, 5):
            for n in (0, 1):
                up_pass(t, n)
        for n, g in tile6[TILE6_LEAD:]:
            weight_pass(6, n, g)
        for n in (0, 1):
            up_pass(6, n)
        add_banks(4, result(4, 0, M))
        store(4)
        up_alone(3, 4)
        for n in (0, 1):
            new_bank((7, n), n)
            for g in range(GROUPS):
                weight_pass(7, n, g)
            up_pass(7, n)
        for t in (5, 6):
            add_banks(t, result(t, 0, M))
            store(t)
        add_banks(3, base3)
        store(3)
        for n in (0, 1):
            add_bank(7, n, result(7, 0, M))
            store(7, n * N_TILE, (n + 1) * N_TILE)
